import numpy as np
import ml_dtypes


def mxq(x, axis, fmt="e4m3"):
    dtype, down = {"e4m3": (ml_dtypes.float8_e4m3fn, 7), "e5m2": (ml_dtypes.float8_e5m2, 14)}[fmt]
    v = np.moveaxis(np.asarray(x, np.float32).astype(ml_dtypes.bfloat16).astype(np.float64), axis, -1)
    blocks = v.reshape(v.shape[:-1] + (-1, 32))
    amax = np.abs(blocks).max(-1, keepdims=True)
    byte = np.maximum(np.where(amax > 0, np.frexp(amax)[1] - 1 + 127, 0) - down, 1)
    scale = np.exp2(byte - 127.0)
    codes = (blocks / scale).astype(np.float32).astype(dtype).astype(np.float64)
    return np.moveaxis((codes * scale).reshape(v.shape), -1, axis)


WIDE = False


def mx_kscale(k):
    if not WIDE:
        return np.ones(k)
    levels = np.array([24, -24, 12, -12, 0])
    if k % 512:
        return np.exp2(np.random.permutation(np.resize(levels, k // 32))).repeat(32)
    a = np.empty((k // 512, 16))
    for p in range(k // 512):
        a[p, :8] = np.random.permutation(np.resize(levels, 8))
        for g in range(8):
            far = levels[np.abs(levels - a[p, g]) >= 10]
            a[p, g + 8] = far[np.random.randint(len(far))]
    return np.exp2(a.ravel()).repeat(32)


def f64(x):
    return np.asarray(x).astype(np.float64)


def striped(idx):
    return np.tile(idx.reshape(-1, 16).T, (8, 1)).astype(np.uint16)


def unstriped(offs):
    return offs[:16].T.reshape(-1).astype(np.int64)


E2M1 = np.array([0.0, 0.5, 1.0, 1.5, 2.0, 3.0, 4.0, 6.0, -0.0, -0.5, -1.0, -1.5, -2.0, -3.0, -4.0, -6.0])


def pack_weight(w, fmt):
    k, n = w.shape
    w = f64(np.asarray(w, np.float32).astype(ml_dtypes.bfloat16)).reshape(k // 32, 32, n)
    amax = np.abs(w).max(1)
    if fmt == "e4m3":
        byte = np.frexp(amax)[1] - 1 + 127 - 7
    else:
        mant, ex = np.frexp(amax / 6.0)
        byte = np.where(mant > 0.5, ex, ex - 1) + 127
    byte = np.clip(np.where(amax > 0, byte, 1), 1, 254)
    scaled = (w * np.exp2(127.0 - byte)[:, None, :]).reshape(k, n).astype(np.float32)
    by_word = np.ascontiguousarray(scaled.reshape(k // 512, 128, 4, n).transpose(0, 1, 3, 2))
    if fmt == "e4m3":
        words = by_word.astype(ml_dtypes.float8_e4m3fn).view(np.uint8)
    else:
        c = by_word.astype(ml_dtypes.float4_e2m1fn).view(np.uint8) & 0xF
        words = (c[..., 0::2] | (c[..., 1::2] << 4)).reshape(k // 512, 128, 2 * n)
    return np.ascontiguousarray(words), np.ascontiguousarray(byte.astype(np.uint8).reshape(k // 512, 16, n))


def unpack_weight(words, scales, fmt):
    g, _, n = scales.shape
    words = np.ascontiguousarray(words).reshape(g, 128, n, -1)
    if fmt == "e4m3":
        vals = words.view(ml_dtypes.float8_e4m3fn).astype(np.float64)
    else:
        nib = np.empty((g, 128, n, 4), np.uint8)
        nib[..., 0::2] = words & 0xF
        nib[..., 1::2] = words >> 4
        vals = E2M1[nib]
    vals = vals * np.repeat(np.exp2(scales.astype(np.float64) - 127.0), 8, axis=1)[..., None]
    return vals.transpose(0, 1, 3, 2).reshape(g * 512, n)


def pack_table4(v):
    words, scales = pack_weight(v, "e2m1")
    g, t = words.shape[0] // 2, v.shape[1]
    return np.ascontiguousarray(words.reshape(g, 2, 128, t, 2).transpose(0, 2, 3, 1, 4).reshape(g, 128, t, 4)), scales


def unpack_table4(words, scales):
    g, _, t, _ = words.shape
    return unpack_weight(words.reshape(g, 128, t, 2, 2).transpose(0, 3, 1, 2, 4).reshape(2 * g, 128, 2 * t), scales, "e2m1")


def planes(y):
    n, m = y.shape
    v = y.astype(np.float32).astype(ml_dtypes.bfloat16).astype(np.float64).reshape(n // 32, 32, m)
    top = np.abs(v).max(1)
    byte = np.clip(np.where(top > 0, np.frexp(top)[1] - 1 + 127 - 7, 1), 1, 254)
    codes = (v * np.exp2(127.0 - byte)[:, None, :]).reshape(n, m).astype(np.float32).astype(ml_dtypes.float8_e4m3fn).view(np.uint8)
    words = codes.reshape(n // 512, 128, 4, m).transpose(0, 1, 3, 2)
    return np.ascontiguousarray(words), np.ascontiguousarray(byte.astype(np.uint8).reshape(n // 512, 16, m))


def sigm(f):
    return 1.0 / (1.0 + np.exp(-np.maximum(f, -700.0)))


K, M, N, T, J = 1024, 1024, 1024, 2048, 1024


def setup_inputs():
    n = np.random.standard_normal
    s = mx_kscale(K)[:, None]
    s2 = mx_kscale(M)[:, None]
    h = np.tanh(n((N, T)))
    p_tab = pack_table4(h * s2)
    p_uz = pack_weight(n((M, N)) / np.sqrt(M) / s2, "e2m1")
    p_un = pack_weight(n((M, N)) / np.sqrt(M) / s2, "e2m1")
    return {
        "x": (n((K, J)) * s).astype(np.float32),
        "tab_words": p_tab[0],
        "tab_scales": p_tab[1],
        "wz": (n((K, N)) / np.sqrt(K) / s).astype(np.float32),
        "uz_words": p_uz[0],
        "uz_scales": p_uz[1],
        "wn": (n((K, N)) / np.sqrt(K) / s).astype(np.float32),
        "un_words": p_un[0],
        "un_scales": p_un[1],
        "bz": (0.3 * n(N)).astype(np.float32),
        "bn": (0.3 * n(N)).astype(np.float32),
        "hT": (h).astype(np.float32),
        "wgo": np.tile(np.random.uniform(0.5, 2.0, J), (128, 1)).astype(np.float32),
        "offs": striped(np.random.permutation(T)[:J]),
    }


def reference(x, tab_words, tab_scales, wz, uz_words, uz_scales, wn, un_words, un_scales, bz, bn, hT, wgo, offs):
    idx = unstriped(offs)
    x_ = mxq(f64(x), 0, "e4m3")
    tab_ = unpack_table4(tab_words, tab_scales)[:, idx]
    wz_ = mxq(f64(wz), 0, "e4m3")
    uz_ = unpack_weight(uz_words, uz_scales, "e2m1")
    wn_ = mxq(f64(wn), 0, "e4m3")
    un_ = unpack_weight(un_words, un_scales, "e2m1")
    sz = wz_.T @ x_ + uz_.T @ tab_
    z = sigm(sz + f64(bz)[:, None])
    xn = wn_.T @ x_
    hn = un_.T @ tab_
    cd = np.tanh(xn + f64(bn)[:, None] + z * hn)
    out = np.zeros((N, T))
    out[:, idx] = f64(wgo)[0] * (f64(hT)[:, idx] + z * (cd - f64(hT)[:, idx]))
    return (out,) + planes(out)

@@ -1,0 +1,321 @@
+from contextlib import ExitStack
+
+import concourse.mybir as mybir
+
+K, M, N, T, J = 1024, 1024, 1024, 2048, 1024
+FLOPS = 2 * 2 * (K + M) * N * J
+
+F32 = mybir.dt.float32
+BF16 = mybir.dt.bfloat16
+I32 = mybir.dt.int32
+U32 = mybir.dt.uint32
+U16 = mybir.dt.uint16
+U8 = mybir.dt.uint8
+FP8X4 = mybir.dt.float8_e4m3fn_x4
+FP4X4 = mybir.dt.float4_e2m1fn_x4
+ACT = mybir.ActivationFunctionType
+ALU = mybir.AluOpType
+
+P = 128
+PACK = 4
+SPAN = P * PACK
+PASSES = K // SPAN
+GROUPS = N // SPAN
+HALVES = J // SPAN
+CHUNKS = T // SPAN
+QUADS = 4
+LIST_COLS = SPAN // 16
+
+
+def tile_list_tgn_mguP_kernel(
+    tc, x, tab_words, tab_scales, wz, uz_words, uz_scales, wn, un_words, un_scales, bz, bn, hT, wgo, offs,
+    out_0, out_1, out_2,
+):
+    nc = tc.nc
+    with ExitStack() as ctx:
+        keep = ctx.enter_context(tc.tile_pool(name="keep", bufs=1))
+        ring = ctx.enter_context(tc.tile_pool(name="ring", bufs=4))
+        psum = ctx.enter_context(tc.psum_pool(name="psum", bufs=2))
+
+        def held(shape, dtype, name, tag=None):
+            return keep.tile(shape, dtype, name=name, tag=tag or name, align_bytes=64)
+
+        offsets = keep.tile([P, J // 16], U16, name="offsets")
+        nc.sync.dma_start(offsets[:], offs)
+
+        tab_w = held([P, T], U32, "tab_w")
+        tab_words_i32 = tab_words[0].rearrange("p t b -> p (t b)").bitcast(I32)
+        for c in range(2):
+            cols = slice(c * T // 2, (c + 1) * T // 2)
+            nc.sync.dma_start(tab_w[:].bitcast(I32)[:, cols], tab_words_i32[:, cols])
+        bias = []
+        for w, vec in enumerate((bz, bn)):
+            tile = held([P, GROUPS, PACK], F32, f"bias{w}")
+            nc.sync.dma_start(tile[:], vec.rearrange("(a p t) -> p a t", a=GROUPS, t=PACK))
+            bias.append(tile)
+
+        neg_bz = held([P, GROUPS, PACK], F32, "neg_bz")
+        nc.scalar.activation(neg_bz[:], bias[0][:], ACT.Copy, scale=-1.0)
+
+        tab_s = held([P, PASSES, T], U8, "tab_s")
+        nc.vector.memset(tab_s[:].bitcast(I32), 0)
+        u_s_raw = [held([P, PASSES, N], U8, f"u_s_raw{w}") for w in range(2)]
+        for tile in u_s_raw:
+            nc.vector.memset(tile[:].bitcast(I32), 0)
+        v_s = [held([P, J], U8, f"v_s{k}") for k in range(PASSES)]
+        pages = [held([P, T], F32, f"page{t}") for t in range(PACK)]
+        for page in pages:
+            nc.vector.memset(page[:], 0.0)
+
+        def load_rows(mat, k, c, pieces=1):
+            raw = ring.tile([P, PACK, SPAN], F32, name="raw", tag="raw", align_bytes=64)
+            rows = mat[k * SPAN : (k + 1) * SPAN, c * SPAN : (c + 1) * SPAN].rearrange("(p i) c -> p i c", i=PACK)
+            step = PACK // pieces
+            for i in range(0, PACK, step):
+                nc.sync.dma_start(raw[:, i : i + step, :], rows[:, i : i + step, :])
+            return raw
+
+        def load_scale_rows(tile, scales, rows):
+            for r in rows:
+                nc.sync.dma_start(
+                    tile[r:P:32].bitcast(I32), scales[:, r:16:4, :].rearrange("k q n -> q k n").bitcast(I32)
+                )
+
+        def new_grouped():
+            return ring.tile([P, PACK * SPAN], BF16, name="grouped", tag="grouped", align_bytes=64)
+
+        def weave(copy, src):
+            grouped = new_grouped()
+            copy(
+                out=grouped[:].rearrange("p (c u i) -> p c i u", u=4, i=PACK),
+                in_=src[:].rearrange("p i (c u) -> p c i u", u=4),
+            )
+            return grouped
+
+        def weave_dealt(src):
+            grouped = new_grouped()
+            nc.scalar.copy(
+                out=grouped[:].rearrange("p (t m i) -> p m t i", t=PACK, i=PACK),
+                in_=src[:].rearrange("p i (m t) -> p m t i", t=PACK),
+            )
+            return grouped
+
+        def quantise(grouped, name):
+            codes = held([P, SPAN], U32, name + "_c")
+            scales = held([P, SPAN], U8, name + "_s")
+            nc.vector.quantize_mx(out=codes[:].bitcast(FP8X4), scales=scales[:], in_=grouped[:])
+            return codes, scales
+
+        raw_x = {(0, 0): load_rows(x, 0, 0, pieces=2)}
+        u_w_raw = [held([P, PASSES, 2 * N], U8, f"u_w_raw{w}") for w in range(2)]
+        nc.sync.dma_start(u_w_raw[0][:].bitcast(I32), uz_words.rearrange("k p n -> p k n").bitcast(I32))
+        load_scale_rows(tab_s, tab_scales, range(4))
+        raw_x[1, 0] = load_rows(x, 1, 0)
+        nc.sync.dma_start(u_w_raw[1][:].bitcast(I32), un_words.rearrange("k p n -> p k n").bitcast(I32))
+        load_scale_rows(u_s_raw[0], uz_scales, range(2))
+        raw_w = {(0, 0, 0): load_rows(wz, 0, 0)}
+        load_scale_rows(u_s_raw[0], uz_scales, range(2, 4))
+        raw_w[0, 1, 0] = load_rows(wz, 1, 0)
+        load_scale_rows(u_s_raw[1], un_scales, range(4))
+
+        pair_words = held([P, J], U32, "pair_words")
+        nc.vector.tensor_copy(pair_words[:], tab_w[:].indirect(offsets[:]))
+        v_w = held([P, PASSES, 2 * J], U8, "v_w")
+        nc.vector.tensor_copy(
+            out=v_w[:].bitcast(U16), in_=pair_words[:].bitcast(U16).rearrange("p (j k) -> p k j", k=PASSES)
+        )
+
+        for k in range(PASSES):
+            nc.vector.tensor_copy(v_s[k][:], tab_s[:, k, :].indirect(offsets[:]))
+
+        xq = {}
+        for k in range(PASSES):
+            xq[k, 0] = quantise(weave(nc.scalar.copy, raw_x[k, 0]), f"x{k}0")
+
+        u_w, u_s = [], []
+        for w in range(2):
+            words = held([P, PASSES, 2 * N], U8, f"u_w{w}")
+            nc.vector.tensor_copy(
+                out=words[:].bitcast(U16).rearrange("p k (a t m) -> p (k a) t m", a=GROUPS, t=PACK),
+                in_=u_w_raw[w][:].bitcast(U16).rearrange("p k (a m t) -> p (k a) t m", a=GROUPS, t=PACK),
+            )
+            scales = held([P, PASSES, N], U8, f"u_s{w}")
+            nc.vector.tensor_copy(
+                out=scales[:].rearrange("p k (a t m) -> p (k a) t m", a=GROUPS, t=PACK),
+                in_=u_s_raw[w][:].rearrange("p k (a m t) -> p (k a) t m", a=GROUPS, t=PACK),
+            )
+            u_w.append(words)
+            u_s.append(scales)
+
+        wq = {}
+
+        def prepare_w(w, k, a):
+            wq[w, k, a] = quantise(weave_dealt(load_rows((wz, wn)[w], k, a)), f"w{w}{k}{a}")
+
+        def prepare_x(k, h):
+            xq[k, h] = quantise(weave(nc.scalar.copy, load_rows(x, k, h)), f"x{k}{h}")
+
+        for k in range(PASSES):
+            wq[0, k, 0] = quantise(weave_dealt(raw_w[0, k, 0]), f"w0{k}0")
+        for k in range(PASSES):
+            prepare_w(1, k, 0)
+
+        h_rows = hT.rearrange("(a p t) c -> a t p c", a=GROUPS, t=PACK)
+        out_rows = out_0.rearrange("(a p t) c -> a t p c", a=GROUPS, t=PACK)
+        states = {}
+
+        def load_state(a, t):
+            tile = ring.tile([P, T], F32, name="state", tag="state", align_bytes=64)
+            nc.sync.dma_start(tile[:], h_rows[a, t])
+            states[a, t] = tile
+
+        load_state(0, 0)
+        weight = held([P, J], F32, "weight")
+        nc.sync.dma_start(weight[:], wgo)
+
+        def mx_pass(acc, lhs, rhs, dtype, start, stop):
+            nc.tensor.matmul_mx(
+                out=acc[:], lhsT=lhs[0].bitcast(dtype), lhsT_scale=lhs[1], rhs=rhs[0].bitcast(dtype),
+                rhs_scale=rhs[1], start=start, stop=stop,
+            )
+
+        def message_passes(w, a, t, h):
+            cols = slice(t * P, (t + 1) * P)
+            return [
+                ((wq[w, k, a][0][:, cols], wq[w, k, a][1][:, cols]), (xq[k, h][0][:], xq[k, h][1][:]), FP8X4)
+                for k in range(PASSES)
+            ]
+
+        def state_passes(w, a, t, h):
+            n0 = a * SPAN + t * P
+            j0 = h * SPAN
+            return [
+                (
+                    (u_w[w][:, k, 2 * n0 : 2 * (n0 + P)], u_s[w][:, k, n0 : n0 + P]),
+                    (v_w[:, k, 2 * j0 : 2 * (j0 + SPAN)], v_s[k][:, j0 : j0 + SPAN]),
+                    FP4X4,
+                )
+                for k in range(PASSES)
+            ]
+
+        def product(name, bufs, passes):
+            acc = psum.tile([P, SPAN], F32, name=name, tag=name, bufs=bufs)
+            for i, (lhs, rhs, dtype) in enumerate(passes):
+                mx_pass(acc, lhs, rhs, dtype, i == 0, i == len(passes) - 1)
+            return acc
+
+        units = [(0, t, h) for h in range(HALVES) for t in range(PACK)]
+        units = units + [(1, t, h) for t in range(PACK) for h in range(HALVES)]
+        gate, cand, upd, hn_acc, xn_acc = {}, {}, {}, {}, {}
+
+        def work(name):
+            return ring.tile([P, SPAN], F32, name=name, tag=name, align_bytes=64)
+
+        def products(u):
+            a, t, h = units[u]
+            sz = product("sz", 2, state_passes(0, a, t, h) + message_passes(0, a, t, h))
+            hn_acc[u] = product("hn", 3, state_passes(1, a, t, h))
+            xn_acc[u] = product("xn", 3, message_passes(1, a, t, h))
+            gate[u] = work("gate")
+            nc.scalar.activation(gate[u][:], sz[:], ACT.Sigmoid, bias=neg_bz[:, a, t : t + 1], scale=-1.0)
+
+        def gate_state(u):
+            cand[u] = work("cand")
+            nc.vector.scalar_tensor_tensor(cand[u][:], gate[u][:], 1.0, hn_acc[u][:], ALU.subtract, ALU.mult)
+
+        def candidate(u):
+            a, t, h = units[u]
+            nc.vector.tensor_tensor(cand[u][:], xn_acc[u][:], cand[u][:], ALU.subtract)
+            nc.scalar.activation(cand[u][:], cand[u][:], ACT.Tanh, bias=bias[1][:, a, t : t + 1])
+
+        def entries(h):
+            return offsets[:, h * LIST_COLS : (h + 1) * LIST_COLS]
+
+        def difference(u):
+            a, t, h = units[u]
+            upd[u] = work("upd")
+            nc.vector.tensor_tensor(upd[u][:], states[a, t][:].indirect(entries(h)), cand[u][:], ALU.subtract)
+
+        def blend(u):
+            h = units[u][2]
+            nc.gpsimd.tensor_tensor(upd[u][:], upd[u][:], gate[u][:], ALU.mult)
+            nc.gpsimd.tensor_tensor(upd[u][:], upd[u][:], cand[u][:], ALU.add)
+            nc.gpsimd.tensor_tensor(upd[u][:], upd[u][:], weight[:, h * SPAN : (h + 1) * SPAN], ALU.mult)
+
+        planes = {}
+        plane_tags = ["plane0", "u_w_raw0", "u_w_raw1", "plane3"]
+
+        def round_page(copy, a, t, c):
+            if (a, c) not in planes:
+                planes[a, c] = held([P, PACK, SPAN], BF16, f"plane{a}{c}", tag=plane_tags[c])
+            copy(out=planes[a, c][:, t, :], in_=pages[t][:, c * SPAN : (c + 1) * SPAN])
+
+        def place(u):
+            a, t, h = units[u]
+            nc.vector.tensor_copy(pages[t][:].indirect(entries(h)), upd[u][:])
+            if h == HALVES - 1:
+                nc.sync.dma_start(out_rows[a, t], pages[t][:])
+                if u < len(units) - 1:
+                    for c in range(CHUNKS):
+                        round_page(nc.scalar.copy, a, t, c)
+
+        out_scales = [held([P, T], U8, f"out_s{a}") for a in range(GROUPS)]
+
+        def quantise_out(a, c, grouped):
+            codes = ring.tile([P, SPAN], U32, name="out_c", tag="out_c", align_bytes=64)
+            cols = slice(c * SPAN, (c + 1) * SPAN)
+            nc.vector.quantize_mx(out=codes[:].bitcast(FP8X4), scales=out_scales[a][:, cols], in_=grouped[:])
+            nc.sync.dma_start(out_1[a].rearrange("p t b -> p (t b)").bitcast(I32)[:, cols], codes[:].bitcast(I32))
+
+        def store_scales(a, queues):
+            for q in range(QUADS):
+                queues[q].dma_start(
+                    out_2[a, 4 * q : 4 * q + 4, :].bitcast(I32), out_scales[a][32 * q : 32 * q + 4, :].bitcast(I32)
+                )
+
+        products(0)
+        gate_state(0)
+        candidate(0)
+        for u in range(len(units)):
+            ahead = u + 1 < len(units)
+            if u < PACK - 1:
+                load_state(0, u + 1)
+            if u in (1, 2):
+                prepare_x(u - 1, 1)
+            if 3 <= u < 7:
+                prepare_w((u - 3) // 2, (u - 3) % 2, 1)
+            if ahead:
+                products(u + 1)
+            difference(u)
+            if PACK <= u < 2 * PACK:
+                load_state(1, u - PACK)
+            blend(u)
+            if ahead:
+                gate_state(u + 1)
+                candidate(u + 1)
+            if u > 0:
+                place(u - 1)
+            if u == 2 * PACK:
+                woven = [weave(nc.scalar.copy, planes[0, c]) for c in range(2)]
+            if u == 2 * PACK + 1:
+                for c in range(2):
+                    quantise_out(0, c, woven[c])
+                woven = [weave(nc.scalar.copy, planes[0, c]) for c in range(2, 4)]
+            if u == 2 * PACK + 2:
+                for c in range(2):
+                    quantise_out(0, 2 + c, woven[c])
+                store_scales(0, [nc.sync] * QUADS)
+        place(len(units) - 1)
+        a, t = GROUPS - 1, PACK - 1
+        round_page(nc.scalar.copy, a, t, 2)
+        round_page(nc.vector.tensor_copy, a, t, 0)
+        round_page(nc.vector.tensor_copy, a, t, 1)
+        last = {2: weave(nc.scalar.copy, planes[a, 2])}
+        last[0] = weave(nc.vector.tensor_copy, planes[a, 0])
+        round_page(nc.scalar.copy, a, t, 3)
+        last[1] = weave(nc.vector.tensor_copy, planes[a, 1])
+        quantise_out(a, 0, last[0])
+        last[3] = weave(nc.scalar.copy, planes[a, 3])
+        for c in (1, 2, 3):
+            quantise_out(a, c, last[c])
+        store_scales(a, [nc.sync, nc.scalar, nc.sync, nc.scalar])

@@ -1,6 +1,7 @@
 from contextlib import ExitStack
 
 import concourse.mybir as mybir
+from concourse.masks import make_identity
 
 K, M, N, T, J = 1024, 1024, 1024, 2048, 1024
 FLOPS = 2 * 2 * (K + M) * N * J
@@ -56,6 +57,8 @@ def tile_list_tgn_mguP_kernel(
 
         neg_bz = held([P, GROUPS, PACK], F32, "neg_bz")
         nc.scalar.activation(neg_bz[:], bias[0][:], ACT.Copy, scale=-1.0)
+        identity = held([P, P], F32, "identity")
+        make_identity(nc, identity[:])
 
         tab_s = held([P, PASSES, T], U8, "tab_s")
         nc.vector.memset(tab_s[:].bitcast(I32), 0)
@@ -206,44 +209,56 @@ def tile_list_tgn_mguP_kernel(
 
         units = [(0, t, h) for h in range(HALVES) for t in range(PACK)]
         units = units + [(1, t, h) for t in range(PACK) for h in range(HALVES)]
-        gate, cand, upd, hn_acc, xn_acc = {}, {}, {}, {}, {}
+        gate, keep_gate, message, cand, kept, upd, hn_acc = {}, {}, {}, {}, {}, {}, {}
 
-        def work(name):
-            return ring.tile([P, SPAN], F32, name=name, tag=name, align_bytes=64)
+        def work(name, bufs):
+            return ring.tile([P, SPAN], F32, name=name, tag=name, bufs=bufs, align_bytes=64)
 
         def products(u):
             a, t, h = units[u]
             sz = product("sz", 2, state_passes(0, a, t, h) + message_passes(0, a, t, h))
-            hn_acc[u] = product("hn", 3, state_passes(1, a, t, h))
-            xn_acc[u] = product("xn", 3, message_passes(1, a, t, h))
-            gate[u] = work("gate")
-            nc.scalar.activation(gate[u][:], sz[:], ACT.Sigmoid, bias=neg_bz[:, a, t : t + 1], scale=-1.0)
-
-        def gate_state(u):
-            cand[u] = work("cand")
-            nc.vector.scalar_tensor_tensor(cand[u][:], gate[u][:], 1.0, hn_acc[u][:], ALU.subtract, ALU.mult)
+            hn_acc[u] = product("hn", 2, state_passes(1, a, t, h))
+            xn = product("xn", 1, message_passes(1, a, t, h))
+            gate[u] = work("gate", 3)
+            nc.scalar.activation(gate[u][:], sz[:], ACT.Sigmoid, bias=bias[0][:, a, t : t + 1])
+            message[u] = work("message", 2)
+            nc.scalar.activation(message[u][:], xn[:], ACT.Identity, bias=bias[1][:, a, t : t + 1])
+            keep_gate[u] = work("keep_gate", 2)
+            nc.scalar.activation(keep_gate[u][:], sz[:], ACT.Sigmoid, bias=neg_bz[:, a, t : t + 1], scale=-1.0)
 
         def candidate(u):
-            a, t, h = units[u]
-            nc.vector.tensor_tensor(cand[u][:], xn_acc[u][:], cand[u][:], ALU.subtract)
-            nc.scalar.activation(cand[u][:], cand[u][:], ACT.Tanh, bias=bias[1][:, a, t : t + 1])
+            gated = work("gated", 2)
+            nc.vector.tensor_tensor(gated[:], hn_acc[u][:], gate[u][:], ALU.mult)
+            turned = psum.tile([P, SPAN], F32, name="turned", tag="turned", bufs=1)
+            for j0 in range(0, SPAN, P):
+                for i, term in enumerate((message[u], gated)):
+                    nc.tensor.matmul(
+                        turned[:, j0 : j0 + P], lhsT=term[:, j0 : j0 + P], rhs=identity[:], is_transpose=True,
+                        start=(i == 0), stop=(i == 1),
+                    )
+            cand_turned = work("cand_turned", 1)
+            nc.scalar.activation(cand_turned[:], turned[:], ACT.Tanh)
+            cand[u] = psum.tile([P, SPAN], F32, name="cand", tag="cand", bufs=2)
+            for j0 in range(0, SPAN, P):
+                nc.tensor.transpose(cand[u][:, j0 : j0 + P], cand_turned[:, j0 : j0 + P], identity[:])
 
         def entries(h):
             return offsets[:, h * LIST_COLS : (h + 1) * LIST_COLS]
 
-        def difference(u):
+        def keep_state(u):
             a, t, h = units[u]
-            upd[u] = work("upd")
-            nc.vector.tensor_tensor(upd[u][:], states[a, t][:].indirect(entries(h)), cand[u][:], ALU.subtract)
+            kept[u] = work("kept", 2)
+            nc.vector.tensor_tensor(kept[u][:], states[a, t][:].indirect(entries(h)), keep_gate[u][:], ALU.mult)
+
+        def weigh(u):
+            upd[u] = work("upd", 2)
+            nc.vector.tensor_tensor(upd[u][:], cand[u][:], gate[u][:], ALU.mult)
 
         def blend(u):
-            h = units[u][2]
-            nc.gpsimd.tensor_tensor(upd[u][:], upd[u][:], gate[u][:], ALU.mult)
-            nc.gpsimd.tensor_tensor(upd[u][:], upd[u][:], cand[u][:], ALU.add)
-            nc.gpsimd.tensor_tensor(upd[u][:], upd[u][:], weight[:, h * SPAN : (h + 1) * SPAN], ALU.mult)
+            nc.vector.tensor_tensor(upd[u][:], upd[u][:], kept[u][:], ALU.add)
 
         planes = {}
-        plane_tags = ["plane0", "u_w_raw0", "u_w_raw1", "plane3"]
+        plane_tags = ["tab_w", "u_w_raw0", "u_w_raw1", "tab_s"]
 
         def round_page(copy, a, t, c):
             if (a, c) not in planes:
@@ -252,7 +267,9 @@ def tile_list_tgn_mguP_kernel(
 
         def place(u):
             a, t, h = units[u]
-            nc.vector.tensor_copy(pages[t][:].indirect(entries(h)), upd[u][:])
+            nc.vector.tensor_tensor(
+                pages[t][:].indirect(entries(h)), upd[u][:], weight[:, h * SPAN : (h + 1) * SPAN], ALU.mult
+            )
             if h == HALVES - 1:
                 nc.sync.dma_start(out_rows[a, t], pages[t][:])
                 if u < len(units) - 1:
@@ -274,38 +291,37 @@ def tile_list_tgn_mguP_kernel(
                 )
 
         products(0)
-        gate_state(0)
+        products(1)
         candidate(0)
+        keep_state(0)
         for u in range(len(units)):
-            ahead = u + 1 < len(units)
             if u < PACK - 1:
                 load_state(0, u + 1)
-            if u in (1, 2):
-                prepare_x(u - 1, 1)
-            if 3 <= u < 7:
-                prepare_w((u - 3) // 2, (u - 3) % 2, 1)
-            if ahead:
-                products(u + 1)
-            difference(u)
-            if PACK <= u < 2 * PACK:
-                load_state(1, u - PACK)
-            blend(u)
-            if ahead:
-                gate_state(u + 1)
+            if u in (0, 1):
+                prepare_x(u, 1)
+            if 2 <= u < 6:
+                prepare_w((u - 2) // 2, u % 2, 1)
+            weigh(u)
+            if u + 1 < len(units):
                 candidate(u + 1)
-            if u > 0:
-                place(u - 1)
-            if u == 2 * PACK:
+            if u + 2 < len(units):
+                products(u + 2)
+            blend(u)
+            if u + 1 < len(units):
+                keep_state(u + 1)
+            if PACK - 1 <= u < 2 * PACK - 1:
+                load_state(1, u + 1 - PACK)
+            place(u)
+            if u == 2 * PACK - 1:
                 woven = [weave(nc.scalar.copy, planes[0, c]) for c in range(2)]
-            if u == 2 * PACK + 1:
+            if u == 2 * PACK :
                 for c in range(2):
                     quantise_out(0, c, woven[c])
                 woven = [weave(nc.scalar.copy, planes[0, c]) for c in range(2, 4)]
-            if u == 2 * PACK + 2:
+            if u == 2 * PACK + 1 :
                 for c in range(2):
                     quantise_out(0, 2 + c, woven[c])
                 store_scales(0, [nc.sync] * QUADS)
-        place(len(units) - 1)
         a, t = GROUPS - 1, PACK - 1
         round_page(nc.scalar.copy, a, t, 2)
         round_page(nc.vector.tensor_copy, a, t, 0)

@@ -25,6 +25,8 @@ GROUPS = N // SPAN
 HALVES = J // SPAN
 CHUNKS = T // SPAN
 QUADS = 4
+PIECES = 2
+NP = 2
 LIST_COLS = SPAN // 16
 
 
@@ -44,38 +46,52 @@ def tile_list_tgn_mguP_kernel(
         offsets = keep.tile([P, J // 16], U16, name="offsets")
         nc.sync.dma_start(offsets[:], offs)
 
+        u_words = (uz_words, un_words)
+        u_w_raw = {}
+
+        def load_u_words(w, a):
+            tile = held([P, PASSES, 2 * SPAN], U8, f"u_w_raw{w}{a}")
+            cols = u_words[w].rearrange("k p n -> p k n")[:, :, 2 * a * SPAN : 2 * (a + 1) * SPAN]
+            nc.sync.dma_start(tile[:].bitcast(I32), cols.bitcast(I32))
+            u_w_raw[w, a] = tile
+
+        for w in range(2):
+            load_u_words(w, 0)
         tab_w = held([P, T], U32, "tab_w")
         tab_words_i32 = tab_words[0].rearrange("p t b -> p (t b)").bitcast(I32)
         for c in range(2):
             cols = slice(c * T // 2, (c + 1) * T // 2)
             nc.sync.dma_start(tab_w[:].bitcast(I32)[:, cols], tab_words_i32[:, cols])
-        bias = []
+        neg_bias = []
         for w, vec in enumerate((bz, bn)):
             tile = held([P, GROUPS, PACK], F32, f"bias{w}")
             nc.sync.dma_start(tile[:], vec.rearrange("(a p t) -> p a t", a=GROUPS, t=PACK))
-            bias.append(tile)
-
-        neg_bz = held([P, GROUPS, PACK], F32, "neg_bz")
-        nc.scalar.activation(neg_bz[:], bias[0][:], ACT.Copy, scale=-1.0)
+            neg_bias.append(held([P, GROUPS, PACK], F32, f"neg_bias{w}"))
+            nc.scalar.activation(neg_bias[w][:], tile[:], ACT.Copy, scale=-1.0)
         identity = held([P, P], F32, "identity")
         make_identity(nc, identity[:])
 
         tab_s = held([P, PASSES, T], U8, "tab_s")
-        nc.vector.memset(tab_s[:].bitcast(I32), 0)
         u_s_raw = [held([P, PASSES, N], U8, f"u_s_raw{w}") for w in range(2)]
-        for tile in u_s_raw:
+        for tile in [tab_s] + u_s_raw:
             nc.vector.memset(tile[:].bitcast(I32), 0)
-        v_s = [held([P, J], U8, f"v_s{k}") for k in range(PASSES)]
-        pages = [held([P, T], F32, f"page{t}") for t in range(PACK)]
+        pages = [held([P, T], F32, f"page{t}") for t in range(2)]
         for page in pages:
             nc.vector.memset(page[:], 0.0)
 
-        def load_rows(mat, k, c, pieces=1):
-            raw = ring.tile([P, PACK, SPAN], F32, name="raw", tag="raw", align_bytes=64)
+        def load_rows(mat, k, c, pieces=PIECES, between=None, tag=None):
+            if tag == "state":
+                raw = ring.tile([P, PACK, SPAN], F32, name="raw", tag=tag, align_bytes=64)
+            elif tag:
+                raw = held([P, PACK, SPAN], F32, "raw", tag)
+            else:
+                raw = ring.tile([P, PACK, SPAN], F32, name="raw", tag="raw", bufs=2, align_bytes=64)
             rows = mat[k * SPAN : (k + 1) * SPAN, c * SPAN : (c + 1) * SPAN].rearrange("(p i) c -> p i c", i=PACK)
             step = PACK // pieces
             for i in range(0, PACK, step):
                 nc.sync.dma_start(raw[:, i : i + step, :], rows[:, i : i + step, :])
+                if between:
+                    load_scale_rows(between[0], between[1], range(i, i + step))
             return raw
 
         def load_scale_rows(tile, scales, rows):
@@ -84,23 +100,23 @@ def tile_list_tgn_mguP_kernel(
                     tile[r:P:32].bitcast(I32), scales[:, r:16:4, :].rearrange("k q n -> q k n").bitcast(I32)
                 )
 
-        def new_grouped():
-            return ring.tile([P, PACK * SPAN], BF16, name="grouped", tag="grouped", align_bytes=64)
+        def new_grouped(tag="grouped", bufs=4):
+            return ring.tile([P, PACK * SPAN], BF16, name="grouped", tag=tag, bufs=bufs, align_bytes=64)
 
-        def weave(copy, src):
-            grouped = new_grouped()
-            copy(
-                out=grouped[:].rearrange("p (c u i) -> p c i u", u=4, i=PACK),
-                in_=src[:].rearrange("p i (c u) -> p c i u", u=4),
-            )
+        def weave(copy, src, pieces=1, paced=False):
+            grouped = new_grouped("cand_turned", 2) if paced else new_grouped()
+            dst = grouped[:].rearrange("p (c u i) -> p c i u", u=4, i=PACK)
+            rows = src[:].rearrange("p i (c u) -> p c i u", u=4)
+            for c in range(0, P, P // pieces):
+                copy(out=dst[:, c : c + P // pieces], in_=rows[:, c : c + P // pieces])
             return grouped
 
-        def weave_dealt(src):
-            grouped = new_grouped()
-            nc.scalar.copy(
-                out=grouped[:].rearrange("p (t m i) -> p m t i", t=PACK, i=PACK),
-                in_=src[:].rearrange("p i (m t) -> p m t i", t=PACK),
-            )
+        def weave_dealt(src, name=None, pieces=1):
+            grouped = held([P, PACK * SPAN], BF16, name) if name else new_grouped()
+            dst = grouped[:].rearrange("p (t m i) -> p m t i", t=PACK, i=PACK)
+            rows = src[:].rearrange("p i (m t) -> p m t i", t=PACK)
+            for m in range(0, P, P // pieces):
+                nc.scalar.copy(out=dst[:, m : m + P // pieces], in_=rows[:, m : m + P // pieces])
             return grouped
 
         def quantise(grouped, name):
@@ -109,59 +125,58 @@ def tile_list_tgn_mguP_kernel(
             nc.vector.quantize_mx(out=codes[:].bitcast(FP8X4), scales=scales[:], in_=grouped[:])
             return codes, scales
 
-        raw_x = {(0, 0): load_rows(x, 0, 0, pieces=2)}
-        u_w_raw = [held([P, PASSES, 2 * N], U8, f"u_w_raw{w}") for w in range(2)]
-        nc.sync.dma_start(u_w_raw[0][:].bitcast(I32), uz_words.rearrange("k p n -> p k n").bitcast(I32))
+        raw_x = {(0, 0): load_rows(x, 0, 0, tag="page2")}
         load_scale_rows(tab_s, tab_scales, range(4))
-        raw_x[1, 0] = load_rows(x, 1, 0)
-        nc.sync.dma_start(u_w_raw[1][:].bitcast(I32), un_words.rearrange("k p n -> p k n").bitcast(I32))
-        load_scale_rows(u_s_raw[0], uz_scales, range(2))
-        raw_w = {(0, 0, 0): load_rows(wz, 0, 0)}
-        load_scale_rows(u_s_raw[0], uz_scales, range(2, 4))
+        raw_x[1, 0] = load_rows(x, 1, 0, between=(u_s_raw[0], uz_scales), tag="page3")
+        raw_w = {(0, 0, 0): load_rows(wz, 0, 0, between=(u_s_raw[1], un_scales))}
         raw_w[0, 1, 0] = load_rows(wz, 1, 0)
-        load_scale_rows(u_s_raw[1], un_scales, range(4))
 
+        u_w, u_s = {}, {}
+
+        def deal_u_words(w, a):
+            u_w[w, a] = held([P, PASSES, 2 * SPAN], U8, f"u_w{w}{a}")
+            nc.vector.tensor_copy(
+                out=u_w[w, a][:].bitcast(U16).rearrange("p k (t m) -> p k t m", t=PACK),
+                in_=u_w_raw[w, a][:].bitcast(U16).rearrange("p k (m t) -> p k t m", t=PACK),
+            )
+
+        def deal_u_scales(w, a, tag=None):
+            u_s[w, a] = held([P, PASSES, SPAN], U8, f"u_s{w}{a}", tag)
+            nc.vector.tensor_copy(
+                out=u_s[w, a][:].rearrange("p k (t m) -> p k t m", t=PACK),
+                in_=u_s_raw[w][:, :, a * SPAN : (a + 1) * SPAN].rearrange("p k (m t) -> p k t m", t=PACK),
+            )
+
+        for w in range(2):
+            deal_u_words(w, 0)
         pair_words = held([P, J], U32, "pair_words")
         nc.vector.tensor_copy(pair_words[:], tab_w[:].indirect(offsets[:]))
+        v_s = [held([P, J], U8, f"v_s{k}") for k in range(PASSES)]
+        for k in range(PASSES):
+            nc.vector.tensor_copy(v_s[k][:], tab_s[:, k, :].indirect(offsets[:]))
         v_w = held([P, PASSES, 2 * J], U8, "v_w")
         nc.vector.tensor_copy(
             out=v_w[:].bitcast(U16), in_=pair_words[:].bitcast(U16).rearrange("p (j k) -> p k j", k=PASSES)
         )
-
-        for k in range(PASSES):
-            nc.vector.tensor_copy(v_s[k][:], tab_s[:, k, :].indirect(offsets[:]))
+        for w in range(2):
+            deal_u_scales(w, 0)
 
         xq = {}
         for k in range(PASSES):
             xq[k, 0] = quantise(weave(nc.scalar.copy, raw_x[k, 0]), f"x{k}0")
 
-        u_w, u_s = [], []
-        for w in range(2):
-            words = held([P, PASSES, 2 * N], U8, f"u_w{w}")
-            nc.vector.tensor_copy(
-                out=words[:].bitcast(U16).rearrange("p k (a t m) -> p (k a) t m", a=GROUPS, t=PACK),
-                in_=u_w_raw[w][:].bitcast(U16).rearrange("p k (a m t) -> p (k a) t m", a=GROUPS, t=PACK),
-            )
-            scales = held([P, PASSES, N], U8, f"u_s{w}")
-            nc.vector.tensor_copy(
-                out=scales[:].rearrange("p k (a t m) -> p (k a) t m", a=GROUPS, t=PACK),
-                in_=u_s_raw[w][:].rearrange("p k (a m t) -> p (k a) t m", a=GROUPS, t=PACK),
-            )
-            u_w.append(words)
-            u_s.append(scales)
-
         wq = {}
 
         def prepare_w(w, k, a):
-            wq[w, k, a] = quantise(weave_dealt(load_rows((wz, wn)[w], k, a)), f"w{w}{k}{a}")
+            wq[w, k, a] = quantise(weave_dealt(load_rows((wz, wn)[w], k, a), pieces=NP), f"w{w}{k}{a}")
 
         def prepare_x(k, h):
-            xq[k, h] = quantise(weave(nc.scalar.copy, load_rows(x, k, h)), f"x{k}{h}")
+            xq[k, h] = quantise(weave(nc.scalar.copy, load_rows(x, k, h, tag=f"page{2 + k}"), NP), f"x{k}{h}")
 
         for k in range(PASSES):
             wq[0, k, 0] = quantise(weave_dealt(raw_w[0, k, 0]), f"w0{k}0")
         for k in range(PASSES):
-            prepare_w(1, k, 0)
+            wq[1, k, 0] = quantise(weave_dealt(load_rows(wn, k, 0, tag=("page2", "state")[k]), f"late{k}"), f"w1{k}0")
 
         h_rows = hT.rearrange("(a p t) c -> a t p c", a=GROUPS, t=PACK)
         out_rows = out_0.rearrange("(a p t) c -> a t p c", a=GROUPS, t=PACK)
@@ -175,6 +190,8 @@ def tile_list_tgn_mguP_kernel(
         load_state(0, 0)
         weight = held([P, J], F32, "weight")
         nc.sync.dma_start(weight[:], wgo)
+        for w in range(2):
+            load_u_words(w, 1)
 
         def mx_pass(acc, lhs, rhs, dtype, start, stop):
             nc.tensor.matmul_mx(
@@ -190,11 +207,10 @@ def tile_list_tgn_mguP_kernel(
             ]
 
         def state_passes(w, a, t, h):
-            n0 = a * SPAN + t * P
             j0 = h * SPAN
             return [
                 (
-                    (u_w[w][:, k, 2 * n0 : 2 * (n0 + P)], u_s[w][:, k, n0 : n0 + P]),
+                    (u_w[w, a][:, k, 2 * t * P : 2 * (t + 1) * P], u_s[w, a][:, k, t * P : (t + 1) * P]),
                     (v_w[:, k, 2 * j0 : 2 * (j0 + SPAN)], v_s[k][:, j0 : j0 + SPAN]),
                     FP4X4,
                 )
@@ -209,34 +225,33 @@ def tile_list_tgn_mguP_kernel(
 
         units = [(0, t, h) for h in range(HALVES) for t in range(PACK)]
         units = units + [(1, t, h) for t in range(PACK) for h in range(HALVES)]
-        gate, keep_gate, message, cand, kept, upd, hn_acc = {}, {}, {}, {}, {}, {}, {}
+        gate, message, cand, kept, upd = {}, {}, {}, {}, {}
 
         def work(name, bufs):
             return ring.tile([P, SPAN], F32, name=name, tag=name, bufs=bufs, align_bytes=64)
 
         def products(u):
             a, t, h = units[u]
-            sz = product("sz", 2, state_passes(0, a, t, h) + message_passes(0, a, t, h))
-            hn_acc[u] = product("hn", 2, state_passes(1, a, t, h))
-            xn = product("xn", 1, message_passes(1, a, t, h))
-            gate[u] = work("gate", 3)
-            nc.scalar.activation(gate[u][:], sz[:], ACT.Sigmoid, bias=bias[0][:, a, t : t + 1])
+            sz = product("sz", 2, message_passes(0, a, t, h) + state_passes(0, a, t, h))
+            xn = product("xn", 2, message_passes(1, a, t, h))
+            gate[u] = work("gate", 5)
+            nc.scalar.activation(gate[u][:], sz[:], ACT.Sigmoid, bias=neg_bias[0][:, a, t : t + 1], scale=-1.0)
             message[u] = work("message", 2)
-            nc.scalar.activation(message[u][:], xn[:], ACT.Identity, bias=bias[1][:, a, t : t + 1])
-            keep_gate[u] = work("keep_gate", 2)
-            nc.scalar.activation(keep_gate[u][:], sz[:], ACT.Sigmoid, bias=neg_bz[:, a, t : t + 1], scale=-1.0)
+            nc.scalar.activation(message[u][:], xn[:], ACT.Identity, bias=neg_bias[1][:, a, t : t + 1], scale=-1.0)
 
         def candidate(u):
+            a, t, h = units[u]
+            hn = product("hn", 1, state_passes(1, a, t, h))
             gated = work("gated", 2)
-            nc.vector.tensor_tensor(gated[:], hn_acc[u][:], gate[u][:], ALU.mult)
-            turned = psum.tile([P, SPAN], F32, name="turned", tag="turned", bufs=1)
+            nc.vector.scalar_tensor_tensor(gated[:], gate[u][:], 1.0, hn[:], ALU.subtract, ALU.mult)
+            turned = psum.tile([P, SPAN], F32, name="turned", tag="hn", bufs=1)
             for j0 in range(0, SPAN, P):
                 for i, term in enumerate((message[u], gated)):
                     nc.tensor.matmul(
                         turned[:, j0 : j0 + P], lhsT=term[:, j0 : j0 + P], rhs=identity[:], is_transpose=True,
                         start=(i == 0), stop=(i == 1),
                     )
-            cand_turned = work("cand_turned", 1)
+            cand_turned = work("cand_turned", 2)
             nc.scalar.activation(cand_turned[:], turned[:], ACT.Tanh)
             cand[u] = psum.tile([P, SPAN], F32, name="cand", tag="cand", bufs=2)
             for j0 in range(0, SPAN, P):
@@ -247,22 +262,21 @@ def tile_list_tgn_mguP_kernel(
 
         def keep_state(u):
             a, t, h = units[u]
-            kept[u] = work("kept", 2)
-            nc.vector.tensor_tensor(kept[u][:], states[a, t][:].indirect(entries(h)), keep_gate[u][:], ALU.mult)
+            kept[u] = gate[u - 1] if u > 0 else work("gate", 5)
+            nc.vector.tensor_tensor(kept[u][:], states[a, t][:].indirect(entries(h)), gate[u][:], ALU.mult)
 
         def weigh(u):
             upd[u] = work("upd", 2)
-            nc.vector.tensor_tensor(upd[u][:], cand[u][:], gate[u][:], ALU.mult)
+            nc.vector.scalar_tensor_tensor(upd[u][:], gate[u][:], 1.0, cand[u][:], ALU.subtract, ALU.mult)
 
         def blend(u):
             nc.vector.tensor_tensor(upd[u][:], upd[u][:], kept[u][:], ALU.add)
 
         planes = {}
-        plane_tags = ["tab_w", "u_w_raw0", "u_w_raw1", "tab_s"]
 
         def round_page(copy, a, t, c):
             if (a, c) not in planes:
-                planes[a, c] = held([P, PACK, SPAN], BF16, f"plane{a}{c}", tag=plane_tags[c])
+                planes[a, c] = held([P, PACK, SPAN], BF16, f"plane{a}{c}", tag=("tab_w", "tab_s", "plane2", "plane3")[c])
             copy(out=planes[a, c][:, t, :], in_=pages[t][:, c * SPAN : (c + 1) * SPAN])
 
         def place(u):
@@ -272,7 +286,7 @@ def tile_list_tgn_mguP_kernel(
             )
             if h == HALVES - 1:
                 nc.sync.dma_start(out_rows[a, t], pages[t][:])
-                if u < len(units) - 1:
+                if u < len(units) - 1 and u != 2 * PACK + 1 and u != 2 * PACK + 3:
                     for c in range(CHUNKS):
                         round_page(nc.scalar.copy, a, t, c)
 
@@ -294,11 +308,16 @@ def tile_list_tgn_mguP_kernel(
         products(1)
         candidate(0)
         keep_state(0)
+        for w in range(2):
+            deal_u_words(w, 1)
+            deal_u_scales(w, 1, f"late{w}")
         for u in range(len(units)):
             if u < PACK - 1:
                 load_state(0, u + 1)
             if u in (0, 1):
                 prepare_x(u, 1)
+                pages.append(held([P, T], F32, f"page{2 + u}"))
+                nc.gpsimd.memset(pages[-1][:], 0.0)
             if 2 <= u < 6:
                 prepare_w((u - 2) // 2, u % 2, 1)
             weigh(u)
@@ -312,26 +331,19 @@ def tile_list_tgn_mguP_kernel(
             if PACK - 1 <= u < 2 * PACK - 1:
                 load_state(1, u + 1 - PACK)
             place(u)
-            if u == 2 * PACK - 1:
-                woven = [weave(nc.scalar.copy, planes[0, c]) for c in range(2)]
-            if u == 2 * PACK :
-                for c in range(2):
-                    quantise_out(0, c, woven[c])
-                woven = [weave(nc.scalar.copy, planes[0, c]) for c in range(2, 4)]
-            if u == 2 * PACK + 1 :
-                for c in range(2):
-                    quantise_out(0, 2 + c, woven[c])
+            if 2 * PACK <= u < 3 * PACK:
+                quantise_out(0, u - 2 * PACK, weave(nc.scalar.copy, planes[0, u - 2 * PACK], NP, True))
+            if u == 3 * PACK - 1:
                 store_scales(0, [nc.sync] * QUADS)
+                for t in range(2):
+                    for c in range(CHUNKS):
+                        round_page(nc.scalar.copy, 1, t, c)
         a, t = GROUPS - 1, PACK - 1
-        round_page(nc.scalar.copy, a, t, 2)
-        round_page(nc.vector.tensor_copy, a, t, 0)
-        round_page(nc.vector.tensor_copy, a, t, 1)
-        last = {2: weave(nc.scalar.copy, planes[a, 2])}
-        last[0] = weave(nc.vector.tensor_copy, planes[a, 0])
-        round_page(nc.scalar.copy, a, t, 3)
-        last[1] = weave(nc.vector.tensor_copy, planes[a, 1])
-        quantise_out(a, 0, last[0])
-        last[3] = weave(nc.scalar.copy, planes[a, 3])
-        for c in (1, 2, 3):
+        for c in (2, 3, 0, 1):
+            round_page(nc.vector.tensor_copy, a, t, c)
+        last = {c: weave(nc.scalar.copy, planes[a, c], 1, c == 3) for c in (2, 3)}
+        for c in (0, 1):
+            last[c] = weave(nc.vector.tensor_copy, planes[a, c])
+        for c in range(CHUNKS):
             quantise_out(a, c, last[c])
         store_scales(a, [nc.sync, nc.scalar, nc.sync, nc.scalar])

@@ -25,9 +25,11 @@ GROUPS = N // SPAN
 HALVES = J // SPAN
 CHUNKS = T // SPAN
 QUADS = 4
-PIECES = 2
-NP = 2
 LIST_COLS = SPAN // 16
+GATE, CAND = 0, 1
+LOAD_PARTS = 2
+WEAVE_PARTS = 2
+GATE_BUFS = 4
 
 
 def tile_list_tgn_mguP_kernel(
@@ -43,25 +45,28 @@ def tile_list_tgn_mguP_kernel(
         def held(shape, dtype, name, tag=None):
             return keep.tile(shape, dtype, name=name, tag=tag or name, align_bytes=64)
 
+        def ringed(shape, dtype, tag, bufs):
+            return ring.tile(shape, dtype, name=tag, tag=tag, bufs=bufs, align_bytes=64)
+
         offsets = keep.tile([P, J // 16], U16, name="offsets")
         nc.sync.dma_start(offsets[:], offs)
 
-        u_words = (uz_words, un_words)
-        u_w_raw = {}
+        u_words_raw = {}
 
         def load_u_words(w, a):
-            tile = held([P, PASSES, 2 * SPAN], U8, f"u_w_raw{w}{a}")
-            cols = u_words[w].rearrange("k p n -> p k n")[:, :, 2 * a * SPAN : 2 * (a + 1) * SPAN]
+            tile = held([P, PASSES, 2 * SPAN], U8, f"u_words_raw{w}{a}")
+            cols = (uz_words, un_words)[w].rearrange("g p n -> p g n")[:, :, 2 * a * SPAN : 2 * (a + 1) * SPAN]
             nc.sync.dma_start(tile[:].bitcast(I32), cols.bitcast(I32))
-            u_w_raw[w, a] = tile
+            u_words_raw[w, a] = tile
 
-        for w in range(2):
+        for w in (GATE, CAND):
             load_u_words(w, 0)
-        tab_w = held([P, T], U32, "tab_w")
+        tab_window = held([P, T], U32, "tab_window")
         tab_words_i32 = tab_words[0].rearrange("p t b -> p (t b)").bitcast(I32)
-        for c in range(2):
-            cols = slice(c * T // 2, (c + 1) * T // 2)
-            nc.sync.dma_start(tab_w[:].bitcast(I32)[:, cols], tab_words_i32[:, cols])
+        for part in range(LOAD_PARTS):
+            cols = slice(part * T // LOAD_PARTS, (part + 1) * T // LOAD_PARTS)
+            nc.sync.dma_start(tab_window[:].bitcast(I32)[:, cols], tab_words_i32[:, cols])
+
         neg_bias = []
         for w, vec in enumerate((bz, bn)):
             tile = held([P, GROUPS, PACK], F32, f"bias{w}")
@@ -71,279 +76,294 @@ def tile_list_tgn_mguP_kernel(
         identity = held([P, P], F32, "identity")
         make_identity(nc, identity[:])
 
-        tab_s = held([P, PASSES, T], U8, "tab_s")
-        u_s_raw = [held([P, PASSES, N], U8, f"u_s_raw{w}") for w in range(2)]
-        for tile in [tab_s] + u_s_raw:
+        tab_scale_window = held([P, PASSES, T], U8, "tab_scale_window")
+        u_scales_raw = [held([P, PASSES, N], U8, f"u_scales_raw{w}") for w in (GATE, CAND)]
+        for tile in [tab_scale_window] + u_scales_raw:
             nc.vector.memset(tile[:].bitcast(I32), 0)
-        pages = [held([P, T], F32, f"page{t}") for t in range(2)]
+        pages = [held([P, T], F32, f"page{t}") for t in range(PACK - 1)]
         for page in pages:
             nc.vector.memset(page[:], 0.0)
-
-        def load_rows(mat, k, c, pieces=PIECES, between=None, tag=None):
-            if tag == "state":
-                raw = ring.tile([P, PACK, SPAN], F32, name="raw", tag=tag, align_bytes=64)
-            elif tag:
-                raw = held([P, PACK, SPAN], F32, "raw", tag)
-            else:
-                raw = ring.tile([P, PACK, SPAN], F32, name="raw", tag="raw", bufs=2, align_bytes=64)
-            rows = mat[k * SPAN : (k + 1) * SPAN, c * SPAN : (c + 1) * SPAN].rearrange("(p i) c -> p i c", i=PACK)
-            step = PACK // pieces
-            for i in range(0, PACK, step):
-                nc.sync.dma_start(raw[:, i : i + step, :], rows[:, i : i + step, :])
-                if between:
-                    load_scale_rows(between[0], between[1], range(i, i + step))
-            return raw
+        last_page_tag = f"page{PACK - 1}"
 
         def load_scale_rows(tile, scales, rows):
             for r in rows:
                 nc.sync.dma_start(
-                    tile[r:P:32].bitcast(I32), scales[:, r:16:4, :].rearrange("k q n -> q k n").bitcast(I32)
+                    tile[r:P:32].bitcast(I32), scales[:, r:16:4, :].rearrange("g q n -> q g n").bitcast(I32)
                 )
 
-        def new_grouped(tag="grouped", bufs=4):
-            return ring.tile([P, PACK * SPAN], BF16, name="grouped", tag=tag, bufs=bufs, align_bytes=64)
+        def staging():
+            return ringed([P, PACK, SPAN], F32, "staging", 3)
 
-        def weave(copy, src, pieces=1, paced=False):
-            grouped = new_grouped("cand_turned", 2) if paced else new_grouped()
-            dst = grouped[:].rearrange("p (c u i) -> p c i u", u=4, i=PACK)
-            rows = src[:].rearrange("p i (c u) -> p c i u", u=4)
-            for c in range(0, P, P // pieces):
-                copy(out=dst[:, c : c + P // pieces], in_=rows[:, c : c + P // pieces])
-            return grouped
+        def load_block(raw, mat, g, b, scale_job=None):
+            rows = mat[g * SPAN : (g + 1) * SPAN, b * SPAN : (b + 1) * SPAN].rearrange("(p i) c -> p i c", i=PACK)
+            step = PACK // LOAD_PARTS
+            for i in range(0, PACK, step):
+                nc.sync.dma_start(raw[:, i : i + step, :], rows[:, i : i + step, :])
+                if scale_job:
+                    load_scale_rows(scale_job[0], scale_job[1], range(i, i + step))
+            return raw
 
-        def weave_dealt(src, name=None, pieces=1):
-            grouped = held([P, PACK * SPAN], BF16, name) if name else new_grouped()
-            dst = grouped[:].rearrange("p (t m i) -> p m t i", t=PACK, i=PACK)
+        def woven_tile():
+            return ringed([P, PACK * SPAN], BF16, "woven", 4)
+
+        def weave(copy, woven, src, parts=1):
+            dst = woven[:].rearrange("p (run e i) -> p run i e", e=4, i=PACK)
+            rows = src[:].rearrange("p i (run e) -> p run i e", e=4)
+            for run in range(0, P, P // parts):
+                copy(out=dst[:, run : run + P // parts], in_=rows[:, run : run + P // parts])
+            return woven
+
+        def weave_dealt(copy, woven, src, parts=1):
+            dst = woven[:].rearrange("p (t m i) -> p m t i", t=PACK, i=PACK)
             rows = src[:].rearrange("p i (m t) -> p m t i", t=PACK)
-            for m in range(0, P, P // pieces):
-                nc.scalar.copy(out=dst[:, m : m + P // pieces], in_=rows[:, m : m + P // pieces])
-            return grouped
+            for m in range(0, P, P // parts):
+                copy(out=dst[:, m : m + P // parts], in_=rows[:, m : m + P // parts])
+            return woven
 
-        def quantise(grouped, name):
-            codes = held([P, SPAN], U32, name + "_c")
-            scales = held([P, SPAN], U8, name + "_s")
-            nc.vector.quantize_mx(out=codes[:].bitcast(FP8X4), scales=scales[:], in_=grouped[:])
+        def quantise(woven, name):
+            codes = held([P, SPAN], U32, name + "_codes")
+            scales = held([P, SPAN], U8, name + "_scales")
+            nc.vector.quantize_mx(out=codes[:].bitcast(FP8X4), scales=scales[:], in_=woven[:])
             return codes, scales
 
-        raw_x = {(0, 0): load_rows(x, 0, 0, tag="page2")}
-        load_scale_rows(tab_s, tab_scales, range(4))
-        raw_x[1, 0] = load_rows(x, 1, 0, between=(u_s_raw[0], uz_scales), tag="page3")
-        raw_w = {(0, 0, 0): load_rows(wz, 0, 0, between=(u_s_raw[1], un_scales))}
-        raw_w[0, 1, 0] = load_rows(wz, 1, 0)
+        raw_x = [load_block(staging(), x, 0, 0)]
+        load_scale_rows(tab_scale_window, tab_scales, range(PACK))
+        raw_x.append(
+            load_block(held([P, PACK, SPAN], F32, "raw_x", last_page_tag), x, 1, 0, (u_scales_raw[GATE], uz_scales))
+        )
+        raw_wz = [load_block(staging(), wz, 0, 0, (u_scales_raw[CAND], un_scales))]
+        raw_wz.append(load_block(staging(), wz, 1, 0))
 
-        u_w, u_s = {}, {}
+        u_words, u_scales = {}, {}
 
         def deal_u_words(w, a):
-            u_w[w, a] = held([P, PASSES, 2 * SPAN], U8, f"u_w{w}{a}")
+            u_words[w, a] = held([P, PASSES, 2 * SPAN], U8, f"u_words{w}{a}")
             nc.vector.tensor_copy(
-                out=u_w[w, a][:].bitcast(U16).rearrange("p k (t m) -> p k t m", t=PACK),
-                in_=u_w_raw[w, a][:].bitcast(U16).rearrange("p k (m t) -> p k t m", t=PACK),
+                out=u_words[w, a][:].bitcast(U16).rearrange("p g (t m) -> p g t m", t=PACK),
+                in_=u_words_raw[w, a][:].bitcast(U16).rearrange("p g (m t) -> p g t m", t=PACK),
             )
 
-        def deal_u_scales(w, a, tag=None):
-            u_s[w, a] = held([P, PASSES, SPAN], U8, f"u_s{w}{a}", tag)
+        def deal_u_scales(w, a, dealt):
+            u_scales[w, a] = dealt
             nc.vector.tensor_copy(
-                out=u_s[w, a][:].rearrange("p k (t m) -> p k t m", t=PACK),
-                in_=u_s_raw[w][:, :, a * SPAN : (a + 1) * SPAN].rearrange("p k (m t) -> p k t m", t=PACK),
+                out=dealt.rearrange("p g (t m) -> p g t m", t=PACK),
+                in_=u_scales_raw[w][:, :, a * SPAN : (a + 1) * SPAN].rearrange("p g (m t) -> p g t m", t=PACK),
             )
 
-        for w in range(2):
+        for w in (GATE, CAND):
             deal_u_words(w, 0)
         pair_words = held([P, J], U32, "pair_words")
-        nc.vector.tensor_copy(pair_words[:], tab_w[:].indirect(offsets[:]))
-        v_s = [held([P, J], U8, f"v_s{k}") for k in range(PASSES)]
-        for k in range(PASSES):
-            nc.vector.tensor_copy(v_s[k][:], tab_s[:, k, :].indirect(offsets[:]))
-        v_w = held([P, PASSES, 2 * J], U8, "v_w")
+        nc.vector.tensor_copy(pair_words[:], tab_window[:].indirect(offsets[:]))
+        v_words = held([P, PASSES, 2 * J], U8, "v_words")
         nc.vector.tensor_copy(
-            out=v_w[:].bitcast(U16), in_=pair_words[:].bitcast(U16).rearrange("p (j k) -> p k j", k=PASSES)
+            out=v_words[:].bitcast(U16), in_=pair_words[:].bitcast(U16).rearrange("p (j g) -> p g j", g=PASSES)
         )
-        for w in range(2):
-            deal_u_scales(w, 0)
+        v_scales = [held([P, J], U8, f"v_scales{g}") for g in range(PASSES)]
+        for g in range(PASSES):
+            nc.vector.tensor_copy(v_scales[g][:], tab_scale_window[:, g, :].indirect(offsets[:]))
+        for w in (GATE, CAND):
+            deal_u_scales(w, 0, held([P, PASSES, SPAN], U8, f"u_scales{w}")[:])
 
-        xq = {}
-        for k in range(PASSES):
-            xq[k, 0] = quantise(weave(nc.scalar.copy, raw_x[k, 0]), f"x{k}0")
+        x_mx, w_mx = {}, {}
+        for g in range(PASSES):
+            x_mx[g, 0] = quantise(weave(nc.scalar.copy, woven_tile(), raw_x[g]), f"x{g}0")
+        for g in range(PASSES):
+            w_mx[GATE, g, 0] = quantise(weave_dealt(nc.scalar.copy, woven_tile(), raw_wz[g]), f"w0{g}0")
+        wn_raw = [staging(), ringed([P, PACK, SPAN], F32, "state", PACK)]
+        wn_tags = ["later_scales", last_page_tag]
+        for g in range(PASSES):
+            load_block(wn_raw[g], wn, g, 0)
+            woven = held([P, PACK * SPAN], BF16, f"wn_woven{g}", wn_tags[g])
+            w_mx[CAND, g, 0] = quantise(weave_dealt(nc.vector.tensor_copy, woven, wn_raw[g]), f"w1{g}0")
 
-        wq = {}
+        def prepare_x(g, h):
+            raw = load_block(staging(), x, g, h)
+            x_mx[g, h] = quantise(weave(nc.scalar.copy, woven_tile(), raw, WEAVE_PARTS), f"x{g}{h}")
 
-        def prepare_w(w, k, a):
-            wq[w, k, a] = quantise(weave_dealt(load_rows((wz, wn)[w], k, a), pieces=NP), f"w{w}{k}{a}")
+        def prepare_w(w, g, a):
+            raw = load_block(staging(), (wz, wn)[w], g, a)
+            w_mx[w, g, a] = quantise(weave_dealt(nc.scalar.copy, woven_tile(), raw, WEAVE_PARTS), f"w{w}{g}{a}")
 
-        def prepare_x(k, h):
-            xq[k, h] = quantise(weave(nc.scalar.copy, load_rows(x, k, h, tag=f"page{2 + k}"), NP), f"x{k}{h}")
-
-        for k in range(PASSES):
-            wq[0, k, 0] = quantise(weave_dealt(raw_w[0, k, 0]), f"w0{k}0")
-        for k in range(PASSES):
-            wq[1, k, 0] = quantise(weave_dealt(load_rows(wn, k, 0, tag=("page2", "state")[k]), f"late{k}"), f"w1{k}0")
-
-        h_rows = hT.rearrange("(a p t) c -> a t p c", a=GROUPS, t=PACK)
+        state_rows = hT.rearrange("(a p t) c -> a t p c", a=GROUPS, t=PACK)
         out_rows = out_0.rearrange("(a p t) c -> a t p c", a=GROUPS, t=PACK)
         states = {}
 
         def load_state(a, t):
-            tile = ring.tile([P, T], F32, name="state", tag="state", align_bytes=64)
-            nc.sync.dma_start(tile[:], h_rows[a, t])
-            states[a, t] = tile
+            states[a, t] = ringed([P, T], F32, "state", PACK)
+            nc.sync.dma_start(states[a, t][:], state_rows[a, t])
 
         load_state(0, 0)
         weight = held([P, J], F32, "weight")
         nc.sync.dma_start(weight[:], wgo)
-        for w in range(2):
+        for w in (GATE, CAND):
             load_u_words(w, 1)
-
-        def mx_pass(acc, lhs, rhs, dtype, start, stop):
-            nc.tensor.matmul_mx(
-                out=acc[:], lhsT=lhs[0].bitcast(dtype), lhsT_scale=lhs[1], rhs=rhs[0].bitcast(dtype),
-                rhs_scale=rhs[1], start=start, stop=stop,
-            )
 
         def message_passes(w, a, t, h):
             cols = slice(t * P, (t + 1) * P)
             return [
-                ((wq[w, k, a][0][:, cols], wq[w, k, a][1][:, cols]), (xq[k, h][0][:], xq[k, h][1][:]), FP8X4)
-                for k in range(PASSES)
+                (w_mx[w, g, a][0][:, cols], w_mx[w, g, a][1][:, cols], x_mx[g, h][0][:], x_mx[g, h][1][:], FP8X4)
+                for g in range(PASSES)
             ]
 
         def state_passes(w, a, t, h):
             j0 = h * SPAN
             return [
                 (
-                    (u_w[w, a][:, k, 2 * t * P : 2 * (t + 1) * P], u_s[w, a][:, k, t * P : (t + 1) * P]),
-                    (v_w[:, k, 2 * j0 : 2 * (j0 + SPAN)], v_s[k][:, j0 : j0 + SPAN]),
+                    u_words[w, a][:, g, 2 * t * P : 2 * (t + 1) * P],
+                    u_scales[w, a][:, g, t * P : (t + 1) * P],
+                    v_words[:, g, 2 * j0 : 2 * (j0 + SPAN)],
+                    v_scales[g][:, j0 : j0 + SPAN],
                     FP4X4,
                 )
-                for k in range(PASSES)
+                for g in range(PASSES)
             ]
 
-        def product(name, bufs, passes):
-            acc = psum.tile([P, SPAN], F32, name=name, tag=name, bufs=bufs)
-            for i, (lhs, rhs, dtype) in enumerate(passes):
-                mx_pass(acc, lhs, rhs, dtype, i == 0, i == len(passes) - 1)
+        def bank(tag, bufs):
+            return psum.tile([P, SPAN], F32, name=tag, tag=tag, bufs=bufs)
+
+        def product(acc, passes):
+            for i, (lhs, lhs_scale, rhs, rhs_scale, dtype) in enumerate(passes):
+                nc.tensor.matmul_mx(
+                    out=acc[:], lhsT=lhs.bitcast(dtype), lhsT_scale=lhs_scale, rhs=rhs.bitcast(dtype),
+                    rhs_scale=rhs_scale, start=(i == 0), stop=(i == len(passes) - 1),
+                )
             return acc
 
         units = [(0, t, h) for h in range(HALVES) for t in range(PACK)]
         units = units + [(1, t, h) for t in range(PACK) for h in range(HALVES)]
-        gate, message, cand, kept, upd = {}, {}, {}, {}, {}
+        per_group = PACK * HALVES
+        keep_gate, neg_message, neg_cand, kept, update = {}, {}, {}, {}, {}
 
-        def work(name, bufs):
-            return ring.tile([P, SPAN], F32, name=name, tag=name, bufs=bufs, align_bytes=64)
+        def work(tag, bufs):
+            return ringed([P, SPAN], F32, tag, bufs)
 
-        def products(u):
+        def gate_and_message(u):
             a, t, h = units[u]
-            sz = product("sz", 2, message_passes(0, a, t, h) + state_passes(0, a, t, h))
-            xn = product("xn", 2, message_passes(1, a, t, h))
-            gate[u] = work("gate", 5)
-            nc.scalar.activation(gate[u][:], sz[:], ACT.Sigmoid, bias=neg_bias[0][:, a, t : t + 1], scale=-1.0)
-            message[u] = work("message", 2)
-            nc.scalar.activation(message[u][:], xn[:], ACT.Identity, bias=neg_bias[1][:, a, t : t + 1], scale=-1.0)
+            sz = product(bank("sz", 2), message_passes(GATE, a, t, h) + state_passes(GATE, a, t, h))
+            xn = product(bank("xn", 2), message_passes(CAND, a, t, h))
+            keep_gate[u] = work("keep_gate", GATE_BUFS)
+            nc.scalar.activation(
+                keep_gate[u][:], sz[:], ACT.Sigmoid, bias=neg_bias[GATE][:, a, t : t + 1], scale=-1.0
+            )
+            neg_message[u] = work("neg_message", 2)
+            nc.scalar.activation(
+                neg_message[u][:], xn[:], ACT.Identity, bias=neg_bias[CAND][:, a, t : t + 1], scale=-1.0
+            )
 
         def candidate(u):
             a, t, h = units[u]
-            hn = product("hn", 1, state_passes(1, a, t, h))
-            gated = work("gated", 2)
-            nc.vector.scalar_tensor_tensor(gated[:], gate[u][:], 1.0, hn[:], ALU.subtract, ALU.mult)
-            turned = psum.tile([P, SPAN], F32, name="turned", tag="hn", bufs=1)
+            hn = product(bank("hn", 1), state_passes(CAND, a, t, h))
+            neg_gated = work("neg_gated", 2)
+            nc.vector.scalar_tensor_tensor(neg_gated[:], keep_gate[u][:], 1.0, hn[:], ALU.subtract, ALU.mult)
+            turned_sum = bank("hn", 1)
             for j0 in range(0, SPAN, P):
-                for i, term in enumerate((message[u], gated)):
+                for i, term in enumerate((neg_message[u], neg_gated)):
                     nc.tensor.matmul(
-                        turned[:, j0 : j0 + P], lhsT=term[:, j0 : j0 + P], rhs=identity[:], is_transpose=True,
+                        turned_sum[:, j0 : j0 + P], lhsT=term[:, j0 : j0 + P], rhs=identity[:], is_transpose=True,
                         start=(i == 0), stop=(i == 1),
                     )
-            cand_turned = work("cand_turned", 2)
-            nc.scalar.activation(cand_turned[:], turned[:], ACT.Tanh)
-            cand[u] = psum.tile([P, SPAN], F32, name="cand", tag="cand", bufs=2)
+            turned_cand = work("turned_cand", 2)
+            nc.scalar.activation(turned_cand[:], turned_sum[:], ACT.Tanh)
+            neg_cand[u] = bank("neg_cand", 2)
             for j0 in range(0, SPAN, P):
-                nc.tensor.transpose(cand[u][:, j0 : j0 + P], cand_turned[:, j0 : j0 + P], identity[:])
+                nc.tensor.transpose(neg_cand[u][:, j0 : j0 + P], turned_cand[:, j0 : j0 + P], identity[:])
 
         def entries(h):
             return offsets[:, h * LIST_COLS : (h + 1) * LIST_COLS]
 
         def keep_state(u):
             a, t, h = units[u]
-            kept[u] = gate[u - 1] if u > 0 else work("gate", 5)
-            nc.vector.tensor_tensor(kept[u][:], states[a, t][:].indirect(entries(h)), gate[u][:], ALU.mult)
+            kept[u] = keep_gate[u - 1] if u > 0 else work("keep_gate", GATE_BUFS)
+            nc.vector.tensor_tensor(kept[u][:], states[a, t][:].indirect(entries(h)), keep_gate[u][:], ALU.mult)
 
         def weigh(u):
-            upd[u] = work("upd", 2)
-            nc.vector.scalar_tensor_tensor(upd[u][:], gate[u][:], 1.0, cand[u][:], ALU.subtract, ALU.mult)
+            update[u] = work("update", 2)
+            nc.vector.scalar_tensor_tensor(update[u][:], keep_gate[u][:], 1.0, neg_cand[u][:], ALU.subtract, ALU.mult)
 
         def blend(u):
-            nc.vector.tensor_tensor(upd[u][:], upd[u][:], kept[u][:], ALU.add)
-
-        planes = {}
-
-        def round_page(copy, a, t, c):
-            if (a, c) not in planes:
-                planes[a, c] = held([P, PACK, SPAN], BF16, f"plane{a}{c}", tag=("tab_w", "tab_s", "plane2", "plane3")[c])
-            copy(out=planes[a, c][:, t, :], in_=pages[t][:, c * SPAN : (c + 1) * SPAN])
+            nc.vector.tensor_tensor(update[u][:], update[u][:], kept[u][:], ALU.add)
 
         def place(u):
             a, t, h = units[u]
             nc.vector.tensor_tensor(
-                pages[t][:].indirect(entries(h)), upd[u][:], weight[:, h * SPAN : (h + 1) * SPAN], ALU.mult
+                pages[t][:].indirect(entries(h)), update[u][:], weight[:, h * SPAN : (h + 1) * SPAN], ALU.mult
             )
             if h == HALVES - 1:
                 nc.sync.dma_start(out_rows[a, t], pages[t][:])
-                if u < len(units) - 1 and u != 2 * PACK + 1 and u != 2 * PACK + 3:
-                    for c in range(CHUNKS):
-                        round_page(nc.scalar.copy, a, t, c)
 
-        out_scales = [held([P, T], U8, f"out_s{a}") for a in range(GROUPS)]
+        rounded = {}
+        rounded_tags = ["tab_window", "tab_scale_window", "rounded2", "rounded3"]
+        out_scales = [held([P, T], U8, f"out_scales{a}") for a in range(GROUPS)]
 
-        def quantise_out(a, c, grouped):
-            codes = ring.tile([P, SPAN], U32, name="out_c", tag="out_c", align_bytes=64)
+        def round_page(copy, a, t, chunks):
+            for c in chunks:
+                if (a, c) not in rounded:
+                    rounded[a, c] = held([P, PACK, SPAN], BF16, f"rounded{a}{c}", rounded_tags[c])
+                copy(out=rounded[a, c][:, t, :], in_=pages[t][:, c * SPAN : (c + 1) * SPAN])
+
+        def paced_woven_tile():
+            return ringed([P, PACK * SPAN], BF16, "turned_cand", 2)
+
+        def quantise_out(a, c, woven):
+            codes = ringed([P, SPAN], U32, "out_codes", CHUNKS)
             cols = slice(c * SPAN, (c + 1) * SPAN)
-            nc.vector.quantize_mx(out=codes[:].bitcast(FP8X4), scales=out_scales[a][:, cols], in_=grouped[:])
+            nc.vector.quantize_mx(out=codes[:].bitcast(FP8X4), scales=out_scales[a][:, cols], in_=woven[:])
             nc.sync.dma_start(out_1[a].rearrange("p t b -> p (t b)").bitcast(I32)[:, cols], codes[:].bitcast(I32))
 
         def store_scales(a, queues):
             for q in range(QUADS):
-                queues[q].dma_start(
+                queues[q % len(queues)].dma_start(
                     out_2[a, 4 * q : 4 * q + 4, :].bitcast(I32), out_scales[a][32 * q : 32 * q + 4, :].bitcast(I32)
                 )
 
-        products(0)
-        products(1)
+        gate_and_message(0)
+        gate_and_message(1)
         candidate(0)
         keep_state(0)
-        for w in range(2):
+        for w in (GATE, CAND):
             deal_u_words(w, 1)
-            deal_u_scales(w, 1, f"late{w}")
-        for u in range(len(units)):
-            if u < PACK - 1:
+        later_scales = held([P, 2, PASSES, SPAN], U8, "later_scales")
+        for w in (GATE, CAND):
+            deal_u_scales(w, 1, later_scales[:, w])
+        pages.append(held([P, T], F32, last_page_tag))
+        nc.vector.memset(pages[PACK - 1][:], 0.0)
+
+        later_blocks = [(prepare_x, (g, 1)) for g in range(PASSES)]
+        later_blocks = later_blocks + [(prepare_w, (w, g, 1)) for w in (GATE, CAND) for g in range(PASSES)]
+        weaving_done = per_group + CHUNKS - 1
+        last = len(units) - 1
+        for u, (a, t, h) in enumerate(units):
+            if u + 1 < PACK:
                 load_state(0, u + 1)
-            if u in (0, 1):
-                prepare_x(u, 1)
-                pages.append(held([P, T], F32, f"page{2 + u}"))
-                nc.gpsimd.memset(pages[-1][:], 0.0)
-            if 2 <= u < 6:
-                prepare_w((u - 2) // 2, u % 2, 1)
+            if u < len(later_blocks):
+                later_blocks[u][0](*later_blocks[u][1])
             weigh(u)
-            if u + 1 < len(units):
+            if u + 1 <= last:
                 candidate(u + 1)
-            if u + 2 < len(units):
-                products(u + 2)
+            if u + 2 <= last:
+                gate_and_message(u + 2)
             blend(u)
-            if u + 1 < len(units):
+            if u + 1 <= last:
                 keep_state(u + 1)
-            if PACK - 1 <= u < 2 * PACK - 1:
+            if PACK <= u + 1 < per_group:
                 load_state(1, u + 1 - PACK)
             place(u)
-            if 2 * PACK <= u < 3 * PACK:
-                quantise_out(0, u - 2 * PACK, weave(nc.scalar.copy, planes[0, u - 2 * PACK], NP, True))
-            if u == 3 * PACK - 1:
-                store_scales(0, [nc.sync] * QUADS)
-                for t in range(2):
-                    for c in range(CHUNKS):
-                        round_page(nc.scalar.copy, 1, t, c)
-        a, t = GROUPS - 1, PACK - 1
-        for c in (2, 3, 0, 1):
-            round_page(nc.vector.tensor_copy, a, t, c)
-        last = {c: weave(nc.scalar.copy, planes[a, c], 1, c == 3) for c in (2, 3)}
-        for c in (0, 1):
-            last[c] = weave(nc.vector.tensor_copy, planes[a, c])
+            if h == HALVES - 1 and u < last and not per_group <= u <= weaving_done:
+                round_page(nc.scalar.copy, a, t, range(CHUNKS))
+            if per_group <= u <= weaving_done:
+                c = u - per_group
+                quantise_out(0, c, weave(nc.scalar.copy, paced_woven_tile(), rounded[0, c], WEAVE_PARTS))
+            if u == weaving_done:
+                store_scales(0, [nc.sync])
+                for finished in range(t + 1):
+                    round_page(nc.scalar.copy, 1, finished, range(CHUNKS))
+
+        a = GROUPS - 1
+        vector_chunks, scalar_chunks = (0, 1), (2, 3)
+        round_page(nc.vector.tensor_copy, a, PACK - 1, scalar_chunks + vector_chunks)
+        woven_out = {c: weave(nc.scalar.copy, woven_tile(), rounded[a, c]) for c in scalar_chunks}
+        for c in vector_chunks:
+            woven_out[c] = weave(nc.vector.tensor_copy, woven_tile(), rounded[a, c])
         for c in range(CHUNKS):
-            quantise_out(a, c, last[c])
-        store_scales(a, [nc.sync, nc.scalar, nc.sync, nc.scalar])
+            quantise_out(a, c, woven_out[c])
+        store_scales(a, [nc.sync, nc.scalar])

@@ -29,7 +29,9 @@ LIST_COLS = SPAN // 16
 GATE, CAND = 0, 1
 LOAD_PARTS = 2
 WEAVE_PARTS = 2
-GATE_BUFS = 4
+ROUND_DELAY = 2
+GATE_BUFS = 5
+TURNED_BUFS = 3
 
 
 def tile_list_tgn_mguP_kernel(
@@ -232,15 +234,16 @@ def tile_list_tgn_mguP_kernel(
         units = [(0, t, h) for h in range(HALVES) for t in range(PACK)]
         units = units + [(1, t, h) for t in range(PACK) for h in range(HALVES)]
         per_group = PACK * HALVES
-        keep_gate, neg_message, neg_cand, kept, update = {}, {}, {}, {}, {}
+        keep_gate, neg_message, neg_cand, kept, update, hn, turned_cand = {}, {}, {}, {}, {}, {}, {}
 
         def work(tag, bufs):
             return ringed([P, SPAN], F32, tag, bufs)
 
-        def gate_and_message(u):
+        def products(u):
             a, t, h = units[u]
-            sz = product(bank("sz", 2), message_passes(GATE, a, t, h) + state_passes(GATE, a, t, h))
+            sz = product(bank("sz", 2), state_passes(GATE, a, t, h) + message_passes(GATE, a, t, h))
             xn = product(bank("xn", 2), message_passes(CAND, a, t, h))
+            hn[u] = product(bank("hn", 2), state_passes(CAND, a, t, h))
             keep_gate[u] = work("keep_gate", GATE_BUFS)
             nc.scalar.activation(
                 keep_gate[u][:], sz[:], ACT.Sigmoid, bias=neg_bias[GATE][:, a, t : t + 1], scale=-1.0
@@ -251,29 +254,27 @@ def tile_list_tgn_mguP_kernel(
             )
 
         def candidate(u):
-            a, t, h = units[u]
-            hn = product(bank("hn", 1), state_passes(CAND, a, t, h))
-            neg_gated = work("neg_gated", 2)
-            nc.vector.scalar_tensor_tensor(neg_gated[:], keep_gate[u][:], 1.0, hn[:], ALU.subtract, ALU.mult)
-            turned_sum = bank("hn", 1)
+            neg_gated = keep_gate[u - 2] if u > 1 else work("update", 2)
+            nc.vector.scalar_tensor_tensor(neg_gated[:], keep_gate[u][:], 1.0, hn[u][:], ALU.subtract, ALU.mult)
+            turned_sum = bank("turned_sum", 1)
             for j0 in range(0, SPAN, P):
                 for i, term in enumerate((neg_message[u], neg_gated)):
                     nc.tensor.matmul(
                         turned_sum[:, j0 : j0 + P], lhsT=term[:, j0 : j0 + P], rhs=identity[:], is_transpose=True,
                         start=(i == 0), stop=(i == 1),
                     )
-            turned_cand = work("turned_cand", 2)
-            nc.scalar.activation(turned_cand[:], turned_sum[:], ACT.Tanh)
-            neg_cand[u] = bank("neg_cand", 2)
+            turned_cand[u] = work("turned_cand", TURNED_BUFS)
+            nc.scalar.activation(turned_cand[u][:], turned_sum[:], ACT.Tanh)
+            neg_cand[u] = bank("neg_cand", 1)
             for j0 in range(0, SPAN, P):
-                nc.tensor.transpose(neg_cand[u][:, j0 : j0 + P], turned_cand[:, j0 : j0 + P], identity[:])
+                nc.tensor.transpose(neg_cand[u][:, j0 : j0 + P], turned_cand[u][:, j0 : j0 + P], identity[:])
 
         def entries(h):
             return offsets[:, h * LIST_COLS : (h + 1) * LIST_COLS]
 
         def keep_state(u):
             a, t, h = units[u]
-            kept[u] = keep_gate[u - 1] if u > 0 else work("keep_gate", GATE_BUFS)
+            kept[u] = turned_cand[u - 1] if u > 0 else work("turned_cand", TURNED_BUFS)
             nc.vector.tensor_tensor(kept[u][:], states[a, t][:].indirect(entries(h)), keep_gate[u][:], ALU.mult)
 
         def weigh(u):
@@ -301,9 +302,6 @@ def tile_list_tgn_mguP_kernel(
                     rounded[a, c] = held([P, PACK, SPAN], BF16, f"rounded{a}{c}", rounded_tags[c])
                 copy(out=rounded[a, c][:, t, :], in_=pages[t][:, c * SPAN : (c + 1) * SPAN])
 
-        def paced_woven_tile():
-            return ringed([P, PACK * SPAN], BF16, "turned_cand", 2)
-
         def quantise_out(a, c, woven):
             codes = ringed([P, SPAN], U32, "out_codes", CHUNKS)
             cols = slice(c * SPAN, (c + 1) * SPAN)
@@ -316,10 +314,12 @@ def tile_list_tgn_mguP_kernel(
                     out_2[a, 4 * q : 4 * q + 4, :].bitcast(I32), out_scales[a][32 * q : 32 * q + 4, :].bitcast(I32)
                 )
 
-        gate_and_message(0)
-        gate_and_message(1)
-        candidate(0)
+        products(0)
+        products(1)
         keep_state(0)
+        candidate(0)
+        products(2)
+        candidate(1)
         for w in (GATE, CAND):
             deal_u_words(w, 1)
         later_scales = held([P, 2, PASSES, SPAN], U8, "later_scales")
@@ -330,32 +330,34 @@ def tile_list_tgn_mguP_kernel(
 
         later_blocks = [(prepare_x, (g, 1)) for g in range(PASSES)]
         later_blocks = later_blocks + [(prepare_w, (w, g, 1)) for w in (GATE, CAND) for g in range(PASSES)]
-        weaving_done = per_group + CHUNKS - 1
+        weaving_from = per_group + ROUND_DELAY
+        weaving_done = weaving_from + CHUNKS - 1
         last = len(units) - 1
-        for u, (a, t, h) in enumerate(units):
+        later_blocks[0][0](*later_blocks[0][1])
+        for u in range(len(units)):
             if u + 1 < PACK:
                 load_state(0, u + 1)
-            if u < len(later_blocks):
-                later_blocks[u][0](*later_blocks[u][1])
+            if u + 1 < len(later_blocks):
+                later_blocks[u + 1][0](*later_blocks[u + 1][1])
+            if u + 3 <= last:
+                products(u + 3)
             weigh(u)
-            if u + 1 <= last:
-                candidate(u + 1)
-            if u + 2 <= last:
-                gate_and_message(u + 2)
-            blend(u)
             if u + 1 <= last:
                 keep_state(u + 1)
             if PACK <= u + 1 < per_group:
                 load_state(1, u + 1 - PACK)
+            blend(u)
+            if u + 2 <= last:
+                candidate(u + 2)
             place(u)
-            if h == HALVES - 1 and u < last and not per_group <= u <= weaving_done:
-                round_page(nc.scalar.copy, a, t, range(CHUNKS))
-            if per_group <= u <= weaving_done:
-                c = u - per_group
-                quantise_out(0, c, weave(nc.scalar.copy, paced_woven_tile(), rounded[0, c], WEAVE_PARTS))
+            if PACK <= u - ROUND_DELAY < per_group:
+                round_page(nc.scalar.copy, 0, u - ROUND_DELAY - PACK, range(CHUNKS))
+            if weaving_from <= u <= weaving_done:
+                c = u - weaving_from
+                quantise_out(0, c, weave(nc.scalar.copy, woven_tile(), rounded[0, c], WEAVE_PARTS))
             if u == weaving_done:
                 store_scales(0, [nc.sync])
-                for finished in range(t + 1):
+                for finished in range(PACK - 1):
                     round_page(nc.scalar.copy, 1, finished, range(CHUNKS))
 
         a = GROUPS - 1

from contextlib import ExitStack

import concourse.mybir as mybir
from concourse.masks import make_identity

K, M, N, T, J = 1024, 1024, 1024, 2048, 1024
FLOPS = 2 * 2 * (K + M) * N * J

F32 = mybir.dt.float32
BF16 = mybir.dt.bfloat16
I32 = mybir.dt.int32
U32 = mybir.dt.uint32
U16 = mybir.dt.uint16
U8 = mybir.dt.uint8
FP8X4 = mybir.dt.float8_e4m3fn_x4
FP4X4 = mybir.dt.float4_e2m1fn_x4
ACT = mybir.ActivationFunctionType
ALU = mybir.AluOpType

P = 128
PACK = 4
SPAN = P * PACK
PASSES = K // SPAN
GROUPS = N // SPAN
HALVES = J // SPAN
CHUNKS = T // SPAN
QUADS = 4
LIST_COLS = SPAN // 16
GATE, CAND = 0, 1
LOAD_PARTS = 2
WEAVE_PARTS = 2
ROUND_DELAY = 2
GATE_BUFS = 5
TURNED_BUFS = 3


def tile_list_tgn_mguP_kernel(
    tc, x, tab_words, tab_scales, wz, uz_words, uz_scales, wn, un_words, un_scales, bz, bn, hT, wgo, offs,
    out_0, out_1, out_2,
):
    nc = tc.nc
    with ExitStack() as ctx:
        keep = ctx.enter_context(tc.tile_pool(name="keep", bufs=1))
        ring = ctx.enter_context(tc.tile_pool(name="ring", bufs=4))
        psum = ctx.enter_context(tc.psum_pool(name="psum", bufs=2))

        def held(shape, dtype, name, tag=None):
            return keep.tile(shape, dtype, name=name, tag=tag or name, align_bytes=64)

        def ringed(shape, dtype, tag, bufs):
            return ring.tile(shape, dtype, name=tag, tag=tag, bufs=bufs, align_bytes=64)

        offsets = keep.tile([P, J // 16], U16, name="offsets")
        nc.sync.dma_start(offsets[:], offs)

        u_words_raw = {}

        def load_u_words(w, a):
            tile = held([P, PASSES, 2 * SPAN], U8, f"u_words_raw{w}{a}")
            cols = (uz_words, un_words)[w].rearrange("g p n -> p g n")[:, :, 2 * a * SPAN : 2 * (a + 1) * SPAN]
            nc.sync.dma_start(tile[:].bitcast(I32), cols.bitcast(I32))
            u_words_raw[w, a] = tile

        for w in (GATE, CAND):
            load_u_words(w, 0)
        tab_window = held([P, T], U32, "tab_window")
        tab_words_i32 = tab_words[0].rearrange("p t b -> p (t b)").bitcast(I32)
        for part in range(LOAD_PARTS):
            cols = slice(part * T // LOAD_PARTS, (part + 1) * T // LOAD_PARTS)
            nc.sync.dma_start(tab_window[:].bitcast(I32)[:, cols], tab_words_i32[:, cols])

        neg_bias = []
        for w, vec in enumerate((bz, bn)):
            tile = held([P, GROUPS, PACK], F32, f"bias{w}")
            nc.sync.dma_start(tile[:], vec.rearrange("(a p t) -> p a t", a=GROUPS, t=PACK))
            neg_bias.append(held([P, GROUPS, PACK], F32, f"neg_bias{w}"))
            nc.scalar.activation(neg_bias[w][:], tile[:], ACT.Copy, scale=-1.0)
        identity = held([P, P], F32, "identity")
        make_identity(nc, identity[:])

        tab_scale_window = held([P, PASSES, T], U8, "tab_scale_window")
        u_scales_raw = [held([P, PASSES, N], U8, f"u_scales_raw{w}") for w in (GATE, CAND)]
        for tile in [tab_scale_window] + u_scales_raw:
            nc.vector.memset(tile[:].bitcast(I32), 0)
        pages = [held([P, T], F32, f"page{t}") for t in range(PACK - 1)]
        for page in pages:
            nc.vector.memset(page[:], 0.0)
        last_page_tag = f"page{PACK - 1}"

        def load_scale_rows(tile, scales, rows):
            for r in rows:
                nc.sync.dma_start(
                    tile[r:P:32].bitcast(I32), scales[:, r:16:4, :].rearrange("g q n -> q g n").bitcast(I32)
                )

        def staging():
            return ringed([P, PACK, SPAN], F32, "staging", 3)

        def load_block(raw, mat, g, b, scale_job=None):
            rows = mat[g * SPAN : (g + 1) * SPAN, b * SPAN : (b + 1) * SPAN].rearrange("(p i) c -> p i c", i=PACK)
            step = PACK // LOAD_PARTS
            for i in range(0, PACK, step):
                nc.sync.dma_start(raw[:, i : i + step, :], rows[:, i : i + step, :])
                if scale_job:
                    load_scale_rows(scale_job[0], scale_job[1], range(i, i + step))
            return raw

        def woven_tile():
            return ringed([P, PACK * SPAN], BF16, "woven", 4)

        def weave(copy, woven, src, parts=1):
            dst = woven[:].rearrange("p (run e i) -> p run i e", e=4, i=PACK)
            rows = src[:].rearrange("p i (run e) -> p run i e", e=4)
            for run in range(0, P, P // parts):
                copy(out=dst[:, run : run + P // parts], in_=rows[:, run : run + P // parts])
            return woven

        def weave_dealt(copy, woven, src, parts=1):
            dst = woven[:].rearrange("p (t m i) -> p m t i", t=PACK, i=PACK)
            rows = src[:].rearrange("p i (m t) -> p m t i", t=PACK)
            for m in range(0, P, P // parts):
                copy(out=dst[:, m : m + P // parts], in_=rows[:, m : m + P // parts])
            return woven

        def quantise(woven, name):
            codes = held([P, SPAN], U32, name + "_codes")
            scales = held([P, SPAN], U8, name + "_scales")
            nc.vector.quantize_mx(out=codes[:].bitcast(FP8X4), scales=scales[:], in_=woven[:])
            return codes, scales

        raw_x = [load_block(staging(), x, 0, 0)]
        load_scale_rows(tab_scale_window, tab_scales, range(PACK))
        raw_x.append(
            load_block(held([P, PACK, SPAN], F32, "raw_x", last_page_tag), x, 1, 0, (u_scales_raw[GATE], uz_scales))
        )
        raw_wz = [load_block(staging(), wz, 0, 0, (u_scales_raw[CAND], un_scales))]
        raw_wz.append(load_block(staging(), wz, 1, 0))

        u_words, u_scales = {}, {}

        def deal_u_words(w, a):
            u_words[w, a] = held([P, PASSES, 2 * SPAN], U8, f"u_words{w}{a}")
            nc.vector.tensor_copy(
                out=u_words[w, a][:].bitcast(U16).rearrange("p g (t m) -> p g t m", t=PACK),
                in_=u_words_raw[w, a][:].bitcast(U16).rearrange("p g (m t) -> p g t m", t=PACK),
            )

        def deal_u_scales(w, a, dealt):
            u_scales[w, a] = dealt
            nc.vector.tensor_copy(
                out=dealt.rearrange("p g (t m) -> p g t m", t=PACK),
                in_=u_scales_raw[w][:, :, a * SPAN : (a + 1) * SPAN].rearrange("p g (m t) -> p g t m", t=PACK),
            )

        for w in (GATE, CAND):
            deal_u_words(w, 0)
        pair_words = held([P, J], U32, "pair_words")
        nc.vector.tensor_copy(pair_words[:], tab_window[:].indirect(offsets[:]))
        v_words = held([P, PASSES, 2 * J], U8, "v_words")
        nc.vector.tensor_copy(
            out=v_words[:].bitcast(U16), in_=pair_words[:].bitcast(U16).rearrange("p (j g) -> p g j", g=PASSES)
        )
        v_scales = [held([P, J], U8, f"v_scales{g}") for g in range(PASSES)]
        for g in range(PASSES):
            nc.vector.tensor_copy(v_scales[g][:], tab_scale_window[:, g, :].indirect(offsets[:]))
        for w in (GATE, CAND):
            deal_u_scales(w, 0, held([P, PASSES, SPAN], U8, f"u_scales{w}")[:])

        x_mx, w_mx = {}, {}
        for g in range(PASSES):
            x_mx[g, 0] = quantise(weave(nc.scalar.copy, woven_tile(), raw_x[g]), f"x{g}0")
        for g in range(PASSES):
            w_mx[GATE, g, 0] = quantise(weave_dealt(nc.scalar.copy, woven_tile(), raw_wz[g]), f"w0{g}0")
        wn_raw = [staging(), ringed([P, PACK, SPAN], F32, "state", PACK)]
        wn_tags = ["later_scales", last_page_tag]
        for g in range(PASSES):
            load_block(wn_raw[g], wn, g, 0)
            woven = held([P, PACK * SPAN], BF16, f"wn_woven{g}", wn_tags[g])
            w_mx[CAND, g, 0] = quantise(weave_dealt(nc.vector.tensor_copy, woven, wn_raw[g]), f"w1{g}0")

        def prepare_x(g, h):
            raw = load_block(staging(), x, g, h)
            x_mx[g, h] = quantise(weave(nc.scalar.copy, woven_tile(), raw, WEAVE_PARTS), f"x{g}{h}")

        def prepare_w(w, g, a):
            raw = load_block(staging(), (wz, wn)[w], g, a)
            w_mx[w, g, a] = quantise(weave_dealt(nc.scalar.copy, woven_tile(), raw, WEAVE_PARTS), f"w{w}{g}{a}")

        state_rows = hT.rearrange("(a p t) c -> a t p c", a=GROUPS, t=PACK)
        out_rows = out_0.rearrange("(a p t) c -> a t p c", a=GROUPS, t=PACK)
        states = {}

        def load_state(a, t):
            states[a, t] = ringed([P, T], F32, "state", PACK)
            nc.sync.dma_start(states[a, t][:], state_rows[a, t])

        load_state(0, 0)
        weight = held([P, J], F32, "weight")
        nc.sync.dma_start(weight[:], wgo)
        for w in (GATE, CAND):
            load_u_words(w, 1)

        def message_passes(w, a, t, h):
            cols = slice(t * P, (t + 1) * P)
            return [
                (w_mx[w, g, a][0][:, cols], w_mx[w, g, a][1][:, cols], x_mx[g, h][0][:], x_mx[g, h][1][:], FP8X4)
                for g in range(PASSES)
            ]

        def state_passes(w, a, t, h):
            j0 = h * SPAN
            return [
                (
                    u_words[w, a][:, g, 2 * t * P : 2 * (t + 1) * P],
                    u_scales[w, a][:, g, t * P : (t + 1) * P],
                    v_words[:, g, 2 * j0 : 2 * (j0 + SPAN)],
                    v_scales[g][:, j0 : j0 + SPAN],
                    FP4X4,
                )
                for g in range(PASSES)
            ]

        def bank(tag, bufs):
            return psum.tile([P, SPAN], F32, name=tag, tag=tag, bufs=bufs)

        def product(acc, passes):
            for i, (lhs, lhs_scale, rhs, rhs_scale, dtype) in enumerate(passes):
                nc.tensor.matmul_mx(
                    out=acc[:], lhsT=lhs.bitcast(dtype), lhsT_scale=lhs_scale, rhs=rhs.bitcast(dtype),
                    rhs_scale=rhs_scale, start=(i == 0), stop=(i == len(passes) - 1),
                )
            return acc

        units = [(0, t, h) for h in range(HALVES) for t in range(PACK)]
        units = units + [(1, t, h) for t in range(PACK) for h in range(HALVES)]
        per_group = PACK * HALVES
        keep_gate, neg_message, neg_cand, kept, update, hn, turned_cand = {}, {}, {}, {}, {}, {}, {}

        def work(tag, bufs):
            return ringed([P, SPAN], F32, tag, bufs)

        def products(u):
            a, t, h = units[u]
            sz = product(bank("sz", 2), state_passes(GATE, a, t, h) + message_passes(GATE, a, t, h))
            xn = product(bank("xn", 2), message_passes(CAND, a, t, h))
            hn[u] = product(bank("hn", 2), state_passes(CAND, a, t, h))
            keep_gate[u] = work("keep_gate", GATE_BUFS)
            nc.scalar.activation(
                keep_gate[u][:], sz[:], ACT.Sigmoid, bias=neg_bias[GATE][:, a, t : t + 1], scale=-1.0
            )
            neg_message[u] = work("neg_message", 2)
            nc.scalar.activation(
                neg_message[u][:], xn[:], ACT.Identity, bias=neg_bias[CAND][:, a, t : t + 1], scale=-1.0
            )

        def candidate(u):
            neg_gated = keep_gate[u - 2] if u > 1 else work("update", 2)
            nc.vector.scalar_tensor_tensor(neg_gated[:], keep_gate[u][:], 1.0, hn[u][:], ALU.subtract, ALU.mult)
            turned_sum = bank("turned_sum", 1)
            for j0 in range(0, SPAN, P):
                for i, term in enumerate((neg_message[u], neg_gated)):
                    nc.tensor.matmul(
                        turned_sum[:, j0 : j0 + P], lhsT=term[:, j0 : j0 + P], rhs=identity[:], is_transpose=True,
                        start=(i == 0), stop=(i == 1),
                    )
            turned_cand[u] = work("turned_cand", TURNED_BUFS)
            nc.scalar.activation(turned_cand[u][:], turned_sum[:], ACT.Tanh)
            neg_cand[u] = bank("neg_cand", 1)
            for j0 in range(0, SPAN, P):
                nc.tensor.transpose(neg_cand[u][:, j0 : j0 + P], turned_cand[u][:, j0 : j0 + P], identity[:])

        def entries(h):
            return offsets[:, h * LIST_COLS : (h + 1) * LIST_COLS]

        def keep_state(u):
            a, t, h = units[u]
            kept[u] = turned_cand[u - 1] if u > 0 else work("turned_cand", TURNED_BUFS)
            nc.vector.tensor_tensor(kept[u][:], states[a, t][:].indirect(entries(h)), keep_gate[u][:], ALU.mult)

        def weigh(u):
            update[u] = work("update", 2)
            nc.vector.scalar_tensor_tensor(update[u][:], keep_gate[u][:], 1.0, neg_cand[u][:], ALU.subtract, ALU.mult)

        def blend(u):
            nc.vector.tensor_tensor(update[u][:], update[u][:], kept[u][:], ALU.add)

        def place(u):
            a, t, h = units[u]
            nc.vector.tensor_tensor(
                pages[t][:].indirect(entries(h)), update[u][:], weight[:, h * SPAN : (h + 1) * SPAN], ALU.mult
            )
            if h == HALVES - 1:
                nc.sync.dma_start(out_rows[a, t], pages[t][:])

        rounded = {}
        rounded_tags = ["tab_window", "tab_scale_window", "rounded2", "rounded3"]
        out_scales = [held([P, T], U8, f"out_scales{a}") for a in range(GROUPS)]

        def round_page(copy, a, t, chunks):
            for c in chunks:
                if (a, c) not in rounded:
                    rounded[a, c] = held([P, PACK, SPAN], BF16, f"rounded{a}{c}", rounded_tags[c])
                copy(out=rounded[a, c][:, t, :], in_=pages[t][:, c * SPAN : (c + 1) * SPAN])

        def quantise_out(a, c, woven):
            codes = ringed([P, SPAN], U32, "out_codes", CHUNKS)
            cols = slice(c * SPAN, (c + 1) * SPAN)
            nc.vector.quantize_mx(out=codes[:].bitcast(FP8X4), scales=out_scales[a][:, cols], in_=woven[:])
            nc.sync.dma_start(out_1[a].rearrange("p t b -> p (t b)").bitcast(I32)[:, cols], codes[:].bitcast(I32))

        def store_scales(a, queues):
            for q in range(QUADS):
                queues[q % len(queues)].dma_start(
                    out_2[a, 4 * q : 4 * q + 4, :].bitcast(I32), out_scales[a][32 * q : 32 * q + 4, :].bitcast(I32)
                )

        products(0)
        products(1)
        keep_state(0)
        candidate(0)
        products(2)
        candidate(1)
        for w in (GATE, CAND):
            deal_u_words(w, 1)
        later_scales = held([P, 2, PASSES, SPAN], U8, "later_scales")
        for w in (GATE, CAND):
            deal_u_scales(w, 1, later_scales[:, w])
        pages.append(held([P, T], F32, last_page_tag))
        nc.vector.memset(pages[PACK - 1][:], 0.0)

        later_blocks = [(prepare_x, (g, 1)) for g in range(PASSES)]
        later_blocks = later_blocks + [(prepare_w, (w, g, 1)) for w in (GATE, CAND) for g in range(PASSES)]
        weaving_from = per_group + ROUND_DELAY
        weaving_done = weaving_from + CHUNKS - 1
        last = len(units) - 1
        later_blocks[0][0](*later_blocks[0][1])
        for u in range(len(units)):
            if u + 1 < PACK:
                load_state(0, u + 1)
            if u + 1 < len(later_blocks):
                later_blocks[u + 1][0](*later_blocks[u + 1][1])
            if u + 3 <= last:
                products(u + 3)
            weigh(u)
            if u + 1 <= last:
                keep_state(u + 1)
            if PACK <= u + 1 < per_group:
                load_state(1, u + 1 - PACK)
            blend(u)
            if u + 2 <= last:
                candidate(u + 2)
            place(u)
            if PACK <= u - ROUND_DELAY < per_group:
                round_page(nc.scalar.copy, 0, u - ROUND_DELAY - PACK, range(CHUNKS))
            if weaving_from <= u <= weaving_done:
                c = u - weaving_from
                quantise_out(0, c, weave(nc.scalar.copy, woven_tile(), rounded[0, c], WEAVE_PARTS))
            if u == weaving_done:
                store_scales(0, [nc.sync])
                for finished in range(PACK - 1):
                    round_page(nc.scalar.copy, 1, finished, range(CHUNKS))

        a = GROUPS - 1
        vector_chunks, scalar_chunks = (0, 1), (2, 3)
        round_page(nc.vector.tensor_copy, a, PACK - 1, scalar_chunks + vector_chunks)
        woven_out = {c: weave(nc.scalar.copy, woven_tile(), rounded[a, c]) for c in scalar_chunks}
        for c in vector_chunks:
            woven_out[c] = weave(nc.vector.tensor_copy, woven_tile(), rounded[a, c])
        for c in range(CHUNKS):
            quantise_out(a, c, woven_out[c])
        store_scales(a, [nc.sync, nc.scalar])
